import numpy as np
import ml_dtypes


def mxq(x, axis, fmt="e4m3"):
    dtype, down = {"e4m3": (ml_dtypes.float8_e4m3fn, 7), "e5m2": (ml_dtypes.float8_e5m2, 14)}[fmt]
    v = np.moveaxis(np.asarray(x, np.float32).astype(ml_dtypes.bfloat16).astype(np.float64), axis, -1)
    blocks = v.reshape(v.shape[:-1] + (-1, 32))
    amax = np.abs(blocks).max(-1, keepdims=True)
    byte = np.maximum(np.where(amax > 0, np.frexp(amax)[1] - 1 + 127, 0) - down, 1)
    scale = np.exp2(byte - 127.0)
    codes = (blocks / scale).astype(np.float32).astype(dtype).astype(np.float64)
    return np.moveaxis((codes * scale).reshape(v.shape), -1, axis)


WIDE = False


def mx_kscale(k):
    if not WIDE:
        return np.ones(k)
    levels = np.array([10, -10, 5, -5, 0])
    if k % 512:
        return np.exp2(np.random.permutation(np.resize(levels, k // 32))).repeat(32)
    a = np.empty((k // 512, 16))
    for p in range(k // 512):
        a[p, :8] = np.random.permutation(np.resize(levels, 8))
        for g in range(8):
            far = levels[np.abs(levels - a[p, g]) >= 10]
            a[p, g + 8] = far[np.random.randint(len(far))]
    return np.exp2(a.ravel()).repeat(32)


def f64(x):
    return np.asarray(x).astype(np.float64)


def striped(idx):
    return np.tile(idx.reshape(-1, 16).T, (8, 1)).astype(np.uint16)


def unstriped(offs):
    return offs[:16].T.reshape(-1).astype(np.int64)


def pack_weight(w):
    k, n = w.shape
    w = f64(np.asarray(w, np.float32).astype(ml_dtypes.bfloat16)).reshape(k // 32, 32, n)
    amax = np.abs(w).max(1)
    byte = np.clip(np.where(amax > 0, np.frexp(amax)[1] - 1 + 127 - 7, 1), 1, 254)
    scaled = (w * np.exp2(127.0 - byte)[:, None, :]).reshape(k, n).astype(np.float32)
    words = np.ascontiguousarray(scaled.reshape(k // 512, 128, 4, n).transpose(0, 1, 3, 2)).astype(ml_dtypes.float8_e4m3fn).view(np.uint8)
    return words, np.ascontiguousarray(byte.astype(np.uint8).reshape(k // 512, 16, n))


def unpack_weight(words, scales):
    g, p, n, _ = words.shape
    vals = np.ascontiguousarray(words).view(ml_dtypes.float8_e4m3fn).astype(np.float64) * np.repeat(np.exp2(scales.astype(np.float64) - 127.0), 8, axis=1)[..., None]
    return vals.transpose(0, 1, 3, 2).reshape(g * 512, n)


K, T, S, N, U = 512, 2048, 1024, 256, 1024


def setup_inputs():
    n = np.random.standard_normal
    s = mx_kscale(K)[:, None]
    packed_w1 = pack_weight(n((K, N)) / np.sqrt(K) / s)
    packed_w2 = pack_weight(n((K, N)) / np.sqrt(K) / s)
    packed_w3 = pack_weight(n((K, N)) / np.sqrt(K) / s)
    return {
        "xT": (n((K, T)) * s).astype(np.float32),
        "w1_words": packed_w1[0],
        "w1_scales": packed_w1[1],
        "w2_words": packed_w2[0],
        "w2_scales": packed_w2[1],
        "w3_words": packed_w3[0],
        "w3_scales": packed_w3[1],
        "offs": striped(np.random.permutation(T)[:S]),
        "src": striped(np.random.permutation(S)[(S * np.random.uniform(0, 1, U) ** 4).astype(np.int64)]),
        "dst": striped(np.random.permutation(S)),
    }


def reference(xT, w1_words, w1_scales, w2_words, w2_scales, w3_words, w3_scales, offs, src, dst):
    xq = mxq(f64(xT)[:, unstriped(offs)], 0, "e4m3")
    y = unpack_weight(w1_words, w1_scales).T @ xq
    e = unpack_weight(w2_words, w2_scales).T @ xq
    h = unpack_weight(w3_words, w3_scales).T @ xq
    return (np.tanh(y[:, unstriped(dst)] + e[:, unstriped(src)])) * h[:, unstriped(src)]

@@ -1,0 +1,148 @@
+from contextlib import ExitStack
+
+import concourse.mybir as mybir
+
+K, T, S, N, U = 512, 2048, 1024, 256, 1024
+FLOPS = 3 * 2 * K * N * S
+
+F32 = mybir.dt.float32
+BF16 = mybir.dt.bfloat16
+I32 = mybir.dt.int32
+U32 = mybir.dt.uint32
+U16 = mybir.dt.uint16
+U8 = mybir.dt.uint8
+FP8X4 = mybir.dt.float8_e4m3fn_x4
+ADD = mybir.AluOpType.add
+MULT = mybir.AluOpType.mult
+TANH = mybir.ActivationFunctionType.Tanh
+
+P = 128
+PER_COLUMN = 16
+PIECE = 256
+BANK = 512
+
+CHUNKS = (
+    ((0, 1024, "scalar"), (1024, 512, "vector"), (1536, 512, "vector")),
+    ((0, 512, "scalar"), (512, 512, "scalar"), (1024, 512, "vector"), (1536, 256, "scalar"), (1792, 256, "vector")),
+)
+
+
+def entries(lst, first, count):
+    return lst[:, first // PER_COLUMN : (first + count) // PER_COLUMN]
+
+
+def tile_picked_edgeatt_tanh_e_kernel(
+    tc, xT, w1_words, w1_scales, w2_words, w2_scales, w3_words, w3_scales, offs, src, dst, out
+):
+    nc = tc.nc
+    with ExitStack() as ctx:
+        keep = ctx.enter_context(tc.tile_pool(name="keep", bufs=1))
+        psum = ctx.enter_context(tc.psum_pool(name="psum", bufs=8))
+
+        offs_t = keep.tile([P, S // PER_COLUMN], U16, name="offs_t")
+        src_t = keep.tile([P, U // PER_COLUMN], U16, name="src_t")
+        dst_t = keep.tile([P, U // PER_COLUMN], U16, name="dst_t")
+        nc.sync.dma_start(offs_t[:], offs)
+
+        w_scales = keep.tile([P, 3 * N], U8, name="w_scales", align_bytes=64)
+        nc.gpsimd.memset(w_scales[:].bitcast(I32), 0)
+        for w, scales in enumerate((w1_scales, w2_scales, w3_scales)):
+            for q in range(4):
+                nc.gpsimd.dma_start(
+                    w_scales[32 * q : 32 * q + 4, w * N : (w + 1) * N].bitcast(I32),
+                    scales[0, 4 * q : 4 * q + 4, :].bitcast(I32),
+                )
+
+        x_rows = xT.rearrange("(p j) t -> p j t", j=4)
+        pairs = [keep.tile([P, T], U32, name=f"pairs{u}") for u in range(2)]
+        pieces = S // PIECE
+        picked = [keep.tile([P, 2, PIECE], U32, name=f"picked{i}") for i in range(pieces)]
+        raws = []
+        for u in range(2):
+            for c0, width, eng in CHUNKS[u]:
+                raw = keep.tile([P, 2, width], F32, name=f"raw{u}_{c0}")
+                nc.sync.dma_start(raw[:], x_rows[:, 2 * u : 2 * u + 2, c0 : c0 + width])
+                raws.append(raw)
+
+        w_words = []
+        for w, words in enumerate((w1_words, w2_words, w3_words)):
+            wt = keep.tile([P, N], U32, name=f"w_words{w}", align_bytes=64)
+            nc.sync.dma_start(wt[:].bitcast(I32), words[0].rearrange("p n t -> p (n t)").bitcast(I32))
+            w_words.append(wt)
+        nc.sync.dma_start(dst_t[:], dst)
+        nc.sync.dma_start(src_t[:], src)
+
+        r = 0
+        for u in range(2):
+            for c0, width, eng in CHUNKS[u]:
+                to = pairs[u][:, c0 : c0 + width].bitcast(BF16).rearrange("p (t e) -> p t e", e=2)
+                frm = raws[r][:].rearrange("p e t -> p t e")
+                r = r + 1
+                if eng == "scalar":
+                    nc.scalar.copy(to, frm)
+                else:
+                    nc.vector.tensor_copy(to, frm)
+            for i in range(pieces):
+                nc.vector.tensor_copy(picked[i][:, u, :], pairs[u][:].indirect(entries(offs_t, i * PIECE, PIECE)))
+
+        x_words = keep.tile([P, S], U32, name="x_words", align_bytes=64)
+        x_scales = keep.tile([P, S], U8, name="x_scales", align_bytes=64)
+        for i in range(pieces):
+            woven = keep.tile([P, PIECE, 2], U32, name=f"woven{i}", align_bytes=64)
+            nc.scalar.copy(woven[:], picked[i][:].rearrange("p u n -> p n u"))
+            cols = slice(i * PIECE, (i + 1) * PIECE)
+            nc.vector.quantize_mx(
+                out=x_words[:, cols].bitcast(FP8X4),
+                scales=x_scales[:, cols],
+                in_=woven[:].rearrange("p n u -> p (n u)").bitcast(BF16),
+            )
+
+        def product(w, block, width):
+            res = keep.tile([P, S], F32, name=f"res{w}_{block}")
+            rows = slice(block * P, (block + 1) * P)
+            srows = slice(w * N + block * P, w * N + (block + 1) * P)
+            for c0 in range(0, S, width):
+                cols = slice(c0, c0 + width)
+                acc = psum.tile([P, BANK], F32, name="acc")
+                nc.tensor.matmul_mx(
+                    out=acc[:, :width],
+                    lhsT=w_words[w][:, rows].bitcast(FP8X4),
+                    lhsT_scale=w_scales[:, srows],
+                    rhs=x_words[:, cols].bitcast(FP8X4),
+                    rhs_scale=x_scales[:, cols],
+                    start=True,
+                    stop=True,
+                )
+                nc.scalar.copy(res[:, cols], acc[:, :width])
+            return res
+
+        y0 = product(0, 0, PIECE)
+        e0 = product(1, 0, BANK)
+        y1 = product(0, 1, BANK)
+        e1 = product(1, 1, BANK)
+        h0 = product(2, 0, BANK)
+        h1 = product(2, 1, BANK)
+
+        gates = []
+        for block, (y, e) in enumerate(((y0, e0), (y1, e1))):
+            halves = []
+            for c0 in range(0, U, BANK):
+                at_dst = keep.tile([P, BANK], F32, name=f"at_dst{block}_{c0}")
+                nc.vector.tensor_copy(at_dst[:], y[:].indirect(entries(dst_t, c0, BANK)))
+                halves.append(at_dst)
+            gate = keep.tile([P, U], F32, name=f"gate{block}")
+            for half, c0 in enumerate(range(0, U, BANK)):
+                both = keep.tile([P, BANK], F32, name=f"both{block}_{c0}")
+                nc.vector.tensor_tensor(both[:], e[:].indirect(entries(src_t, c0, BANK)), halves[half][:], ADD)
+                nc.scalar.activation(gate[:, c0 : c0 + BANK], both[:], TANH)
+            gates.append(gate)
+
+        for block, (h, cuts) in enumerate(((h0, (512, 512)), (h1, (512, 384, 128)))):
+            c0 = 0
+            for width in cuts:
+                msg = keep.tile([P, width], F32, name=f"msg{block}_{c0}")
+                nc.vector.tensor_tensor(
+                    msg[:], h[:].indirect(entries(src_t, c0, width)), gates[block][:, c0 : c0 + width], MULT
+                )
+                nc.sync.dma_start(out[block * P : (block + 1) * P, c0 : c0 + width], msg[:])
+                c0 = c0 + width

@@ -22,8 +22,8 @@ PIECE = 256
 BANK = 512
 
 CHUNKS = (
-    ((0, 1024, "scalar"), (1024, 512, "vector"), (1536, 512, "vector")),
-    ((0, 512, "scalar"), (512, 512, "scalar"), (1024, 512, "vector"), (1536, 256, "scalar"), (1792, 256, "vector")),
+    ((0, 1024, 0), (1024, 512, 512), (1536, 512, 192)),
+    ((0, 512, 512), (512, 512, 512), (1024, 512, 0), (1536, 256, 256), (1792, 256, 96)),
 )
 
 
@@ -37,21 +37,14 @@ def tile_picked_edgeatt_tanh_e_kernel(
     nc = tc.nc
     with ExitStack() as ctx:
         keep = ctx.enter_context(tc.tile_pool(name="keep", bufs=1))
-        psum = ctx.enter_context(tc.psum_pool(name="psum", bufs=8))
+        psum = ctx.enter_context(tc.psum_pool(name="psum", bufs=1))
 
         offs_t = keep.tile([P, S // PER_COLUMN], U16, name="offs_t")
         src_t = keep.tile([P, U // PER_COLUMN], U16, name="src_t")
         dst_t = keep.tile([P, U // PER_COLUMN], U16, name="dst_t")
-        nc.sync.dma_start(offs_t[:], offs)
 
         w_scales = keep.tile([P, 3 * N], U8, name="w_scales", align_bytes=64)
-        nc.gpsimd.memset(w_scales[:].bitcast(I32), 0)
-        for w, scales in enumerate((w1_scales, w2_scales, w3_scales)):
-            for q in range(4):
-                nc.gpsimd.dma_start(
-                    w_scales[32 * q : 32 * q + 4, w * N : (w + 1) * N].bitcast(I32),
-                    scales[0, 4 * q : 4 * q + 4, :].bitcast(I32),
-                )
+        nc.vector.memset(w_scales[:].bitcast(I32), 0)
 
         x_rows = xT.rearrange("(p j) t -> p j t", j=4)
         pairs = [keep.tile([P, T], U32, name=f"pairs{u}") for u in range(2)]
@@ -63,14 +56,22 @@ def tile_picked_edgeatt_tanh_e_kernel(
                 raw = keep.tile([P, 2, width], F32, name=f"raw{u}_{c0}")
                 nc.sync.dma_start(raw[:], x_rows[:, 2 * u : 2 * u + 2, c0 : c0 + width])
                 raws.append(raw)
+            if u == 0:
+                nc.sync.dma_start(offs_t[:], offs)
 
         w_words = []
-        for w, words in enumerate((w1_words, w2_words, w3_words)):
+        weights = ((w1_words, w1_scales, dst_t, dst), (w2_words, w2_scales, src_t, src), (w3_words, w3_scales, None, None))
+        for w, (words, scales, list_t, lst) in enumerate(weights):
             wt = keep.tile([P, N], U32, name=f"w_words{w}", align_bytes=64)
             nc.sync.dma_start(wt[:].bitcast(I32), words[0].rearrange("p n t -> p (n t)").bitcast(I32))
             w_words.append(wt)
-        nc.sync.dma_start(dst_t[:], dst)
-        nc.sync.dma_start(src_t[:], src)
+            for q in range(4):
+                nc.sync.dma_start(
+                    w_scales[32 * q : 32 * q + 4, w * N : (w + 1) * N].bitcast(I32),
+                    scales[0, 4 * q : 4 * q + 4, :].bitcast(I32),
+                )
+            if list_t is not None:
+                nc.sync.dma_start(list_t[:], lst)
 
         r = 0
         for u in range(2):
@@ -78,10 +79,10 @@ def tile_picked_edgeatt_tanh_e_kernel(
                 to = pairs[u][:, c0 : c0 + width].bitcast(BF16).rearrange("p (t e) -> p t e", e=2)
                 frm = raws[r][:].rearrange("p e t -> p t e")
                 r = r + 1
-                if eng == "scalar":
-                    nc.scalar.copy(to, frm)
-                else:
-                    nc.vector.tensor_copy(to, frm)
+                if eng > 0:
+                    nc.scalar.copy(to[:, :eng, :], frm[:, :eng, :])
+                if eng < width:
+                    nc.vector.tensor_copy(to[:, eng:, :], frm[:, eng:, :])
             for i in range(pieces):
                 nc.vector.tensor_copy(picked[i][:, u, :], pairs[u][:].indirect(entries(offs_t, i * PIECE, PIECE)))
 
@@ -103,7 +104,10 @@ def tile_picked_edgeatt_tanh_e_kernel(
             srows = slice(w * N + block * P, w * N + (block + 1) * P)
             for c0 in range(0, S, width):
                 cols = slice(c0, c0 + width)
-                acc = psum.tile([P, BANK], F32, name="acc")
+                if width == PIECE and c0 < BANK:
+                    acc = psum.tile([P, BANK], F32, name=f"early{c0}")
+                else:
+                    acc = psum.tile([P, BANK], F32, name="acc", bufs=2)
                 nc.tensor.matmul_mx(
                     out=acc[:, :width],
                     lhsT=w_words[w][:, rows].bitcast(FP8X4),
@@ -137,7 +141,7 @@ def tile_picked_edgeatt_tanh_e_kernel(
                 nc.scalar.activation(gate[:, c0 : c0 + BANK], both[:], TANH)
             gates.append(gate)
 
-        for block, (h, cuts) in enumerate(((h0, (512, 512)), (h1, (512, 384, 128)))):
+        for block, (h, cuts) in enumerate(((h0, (512, 512)), (h1, (512, 256, 128, 128)))):
             c0 = 0
             for width in cuts:
                 msg = keep.tile([P, width], F32, name=f"msg{block}_{c0}")

@@ -23,7 +23,7 @@ BANK = 512
 
 CHUNKS = (
     ((0, 1024, 0), (1024, 512, 512), (1536, 512, 192)),
-    ((0, 512, 512), (512, 512, 512), (1024, 512, 0), (1536, 256, 256), (1792, 256, 96)),
+    ((0, 1024, 704), (1024, 512, 0), (1536, 256, 256), (1792, 256, 80)),
 )
 
 
@@ -91,20 +91,23 @@ def tile_picked_edgeatt_tanh_e_kernel(
         for i in range(pieces):
             woven = keep.tile([P, PIECE, 2], U32, name=f"woven{i}", align_bytes=64)
             nc.scalar.copy(woven[:], picked[i][:].rearrange("p u n -> p n u"))
-            cols = slice(i * PIECE, (i + 1) * PIECE)
-            nc.vector.quantize_mx(
-                out=x_words[:, cols].bitcast(FP8X4),
-                scales=x_scales[:, cols],
-                in_=woven[:].rearrange("p n u -> p (n u)").bitcast(BF16),
-            )
+            step = PIECE if i < pieces - 1 else PIECE // 2
+            for n0 in range(0, PIECE, step):
+                cols = slice(i * PIECE + n0, i * PIECE + n0 + step)
+                nc.vector.quantize_mx(
+                    out=x_words[:, cols].bitcast(FP8X4),
+                    scales=x_scales[:, cols],
+                    in_=woven[:, n0 : n0 + step, :].rearrange("p n u -> p (n u)").bitcast(BF16),
+                )
 
-        def product(w, block, width):
+        def product(w, block, widths):
             res = keep.tile([P, S], F32, name=f"res{w}_{block}")
             rows = slice(block * P, (block + 1) * P)
             srows = slice(w * N + block * P, w * N + (block + 1) * P)
-            for c0 in range(0, S, width):
+            c0 = 0
+            for width in widths:
                 cols = slice(c0, c0 + width)
-                if width == PIECE and c0 < BANK:
+                if len(widths) > 2 and c0 < 3 * PIECE:
                     acc = psum.tile([P, BANK], F32, name=f"early{c0}")
                 else:
                     acc = psum.tile([P, BANK], F32, name="acc", bufs=2)
@@ -117,15 +120,19 @@ def tile_picked_edgeatt_tanh_e_kernel(
                     start=True,
                     stop=True,
                 )
-                nc.scalar.copy(res[:, cols], acc[:, :width])
+                if len(widths) > 2 and c0 + width == S:
+                    nc.vector.tensor_copy(res[:, cols], acc[:, :width])
+                else:
+                    nc.scalar.copy(res[:, cols], acc[:, :width])
+                c0 = c0 + width
             return res
 
-        y0 = product(0, 0, PIECE)
-        e0 = product(1, 0, BANK)
-        y1 = product(0, 1, BANK)
-        e1 = product(1, 1, BANK)
-        h0 = product(2, 0, BANK)
-        h1 = product(2, 1, BANK)
+        y0 = product(0, 0, (256, 256, 256, 128, 128))
+        e0 = product(1, 0, (BANK, BANK))
+        y1 = product(0, 1, (BANK, BANK))
+        e1 = product(1, 1, (BANK, BANK))
+        h0 = product(2, 0, (BANK, BANK))
+        h1 = product(2, 1, (BANK, BANK))
 
         gates = []
         for block, (y, e) in enumerate(((y0, e0), (y1, e1))):

@@ -17,18 +17,33 @@ MULT = mybir.AluOpType.mult
 TANH = mybir.ActivationFunctionType.Tanh
 
 P = 128
-PER_COLUMN = 16
-PIECE = 256
+PLANES = 4
+ENTRIES_PER_COLUMN = 16
+QUADRANT = 32
+SCALE_ROWS = 4
 BANK = 512
+PIECE = 256
 
-CHUNKS = (
-    ((0, 1024, 0), (1024, 512, 512), (1536, 512, 192)),
-    ((0, 1024, 704), (1024, 512, 0), (1536, 256, 256), (1792, 256, 80)),
+X_LOADS = (
+    ((1024, 0), (512, 512), (512, 192)),
+    ((1024, 704), (512, 0), (256, 256), (256, 80)),
 )
 
+FIRST_WINDOW_CUTS = (PIECE, PIECE, PIECE, PIECE // 2, PIECE // 2)
+WINDOW_CUTS = (BANK, BANK)
 
-def entries(lst, first, count):
-    return lst[:, first // PER_COLUMN : (first + count) // PER_COLUMN]
+SPARE_FOR_COPY = 352
+SPARE_FOR_FUSED = 16
+
+OUT_CUTS = ((U,), (512, 256, 128, 128))
+
+
+def entries(list_tile, first, count):
+    return list_tile[:, first // ENTRIES_PER_COLUMN : (first + count) // ENTRIES_PER_COLUMN]
+
+
+def with_starts(widths):
+    return [(sum(widths[:i]), width) for i, width in enumerate(widths)]
 
 
 def tile_picked_edgeatt_tanh_e_kernel(
@@ -39,121 +54,121 @@ def tile_picked_edgeatt_tanh_e_kernel(
         keep = ctx.enter_context(tc.tile_pool(name="keep", bufs=1))
         psum = ctx.enter_context(tc.psum_pool(name="psum", bufs=1))
 
-        offs_t = keep.tile([P, S // PER_COLUMN], U16, name="offs_t")
-        src_t = keep.tile([P, U // PER_COLUMN], U16, name="src_t")
-        dst_t = keep.tile([P, U // PER_COLUMN], U16, name="dst_t")
+        offs_tile = keep.tile([P, S // ENTRIES_PER_COLUMN], U16, name="offs_tile")
+        src_tile = keep.tile([P, U // ENTRIES_PER_COLUMN], U16, name="src_tile")
+        dst_tile = keep.tile([P, U // ENTRIES_PER_COLUMN], U16, name="dst_tile")
 
         w_scales = keep.tile([P, 3 * N], U8, name="w_scales", align_bytes=64)
         nc.vector.memset(w_scales[:].bitcast(I32), 0)
 
-        x_rows = xT.rearrange("(p j) t -> p j t", j=4)
+        x_planes = xT.rearrange("(p j) t -> p j t", j=PLANES)
         pairs = [keep.tile([P, T], U32, name=f"pairs{u}") for u in range(2)]
-        pieces = S // PIECE
-        picked = [keep.tile([P, 2, PIECE], U32, name=f"picked{i}") for i in range(pieces)]
-        raws = []
-        for u in range(2):
-            for c0, width, eng in CHUNKS[u]:
-                raw = keep.tile([P, 2, width], F32, name=f"raw{u}_{c0}")
-                nc.sync.dma_start(raw[:], x_rows[:, 2 * u : 2 * u + 2, c0 : c0 + width])
-                raws.append(raw)
+        picked = [keep.tile([P, 2, PIECE], U32, name=f"picked{i}") for i in range(S // PIECE)]
+        x_loaded = []
+        for u, loads in enumerate(X_LOADS):
+            for first, width in with_starts([load[0] for load in loads]):
+                raw = keep.tile([P, 2, width], F32, name=f"raw{u}_{first}")
+                nc.sync.dma_start(raw[:], x_planes[:, 2 * u : 2 * u + 2, first : first + width])
+                x_loaded.append(raw)
             if u == 0:
-                nc.sync.dma_start(offs_t[:], offs)
+                nc.sync.dma_start(offs_tile[:], offs)
 
-        w_words = []
-        weights = ((w1_words, w1_scales, dst_t, dst), (w2_words, w2_scales, src_t, src), (w3_words, w3_scales, None, None))
-        for w, (words, scales, list_t, lst) in enumerate(weights):
-            wt = keep.tile([P, N], U32, name=f"w_words{w}", align_bytes=64)
-            nc.sync.dma_start(wt[:].bitcast(I32), words[0].rearrange("p n t -> p (n t)").bitcast(I32))
-            w_words.append(wt)
-            for q in range(4):
+        def load_weight(w, words, scales):
+            codes = keep.tile([P, N], U32, name=f"w_codes{w}", align_bytes=64)
+            nc.sync.dma_start(codes[:].bitcast(I32), words[0].rearrange("p n t -> p (n t)").bitcast(I32))
+            for q in range(P // QUADRANT):
                 nc.sync.dma_start(
-                    w_scales[32 * q : 32 * q + 4, w * N : (w + 1) * N].bitcast(I32),
-                    scales[0, 4 * q : 4 * q + 4, :].bitcast(I32),
+                    w_scales[QUADRANT * q : QUADRANT * q + SCALE_ROWS, w * N : (w + 1) * N].bitcast(I32),
+                    scales[0, SCALE_ROWS * q : SCALE_ROWS * (q + 1), :].bitcast(I32),
                 )
-            if list_t is not None:
-                nc.sync.dma_start(list_t[:], lst)
+            return codes
 
-        r = 0
-        for u in range(2):
-            for c0, width, eng in CHUNKS[u]:
-                to = pairs[u][:, c0 : c0 + width].bitcast(BF16).rearrange("p (t e) -> p t e", e=2)
-                frm = raws[r][:].rearrange("p e t -> p t e")
-                r = r + 1
-                if eng > 0:
-                    nc.scalar.copy(to[:, :eng, :], frm[:, :eng, :])
-                if eng < width:
-                    nc.vector.tensor_copy(to[:, eng:, :], frm[:, eng:, :])
-            for i in range(pieces):
-                nc.vector.tensor_copy(picked[i][:, u, :], pairs[u][:].indirect(entries(offs_t, i * PIECE, PIECE)))
+        w1_codes = load_weight(0, w1_words, w1_scales)
+        nc.sync.dma_start(dst_tile[:], dst)
+        w2_codes = load_weight(1, w2_words, w2_scales)
+        nc.sync.dma_start(src_tile[:], src)
+        w3_codes = load_weight(2, w3_words, w3_scales)
+        w_codes = (w1_codes, w2_codes, w3_codes)
 
-        x_words = keep.tile([P, S], U32, name="x_words", align_bytes=64)
+        loads_done = 0
+        for u, loads in enumerate(X_LOADS):
+            first = 0
+            for width, on_scalar in loads:
+                rounded = pairs[u][:, first : first + width].bitcast(BF16).rearrange("p (t e) -> p t e", e=2)
+                by_node = x_loaded[loads_done][:].rearrange("p e t -> p t e")
+                if on_scalar > 0:
+                    nc.scalar.copy(rounded[:, :on_scalar, :], by_node[:, :on_scalar, :])
+                if on_scalar < width:
+                    nc.vector.tensor_copy(rounded[:, on_scalar:, :], by_node[:, on_scalar:, :])
+                first = first + width
+                loads_done = loads_done + 1
+            for i, piece in enumerate(picked):
+                nc.vector.tensor_copy(piece[:, u, :], pairs[u][:].indirect(entries(offs_tile, i * PIECE, PIECE)))
+
+        x_codes = keep.tile([P, S], U32, name="x_codes", tag="codes_then_gates", align_bytes=64)
         x_scales = keep.tile([P, S], U8, name="x_scales", align_bytes=64)
-        for i in range(pieces):
+        for i, piece in enumerate(picked):
             woven = keep.tile([P, PIECE, 2], U32, name=f"woven{i}", align_bytes=64)
-            nc.scalar.copy(woven[:], picked[i][:].rearrange("p u n -> p n u"))
-            step = PIECE if i < pieces - 1 else PIECE // 2
-            for n0 in range(0, PIECE, step):
-                cols = slice(i * PIECE + n0, i * PIECE + n0 + step)
-                nc.vector.quantize_mx(
-                    out=x_words[:, cols].bitcast(FP8X4),
-                    scales=x_scales[:, cols],
-                    in_=woven[:, n0 : n0 + step, :].rearrange("p n u -> p (n u)").bitcast(BF16),
-                )
+            nc.scalar.copy(woven[:], piece[:].rearrange("p u n -> p n u"))
+            for first, width in with_starts(FIRST_WINDOW_CUTS):
+                if first // PIECE == i:
+                    within = first % PIECE
+                    nc.vector.quantize_mx(
+                        out=x_codes[:, first : first + width].bitcast(FP8X4),
+                        scales=x_scales[:, first : first + width],
+                        in_=woven[:, within : within + width, :].rearrange("p n u -> p (n u)").bitcast(BF16),
+                    )
 
-        def product(w, block, widths):
-            res = keep.tile([P, S], F32, name=f"res{w}_{block}")
-            rows = slice(block * P, (block + 1) * P)
-            srows = slice(w * N + block * P, w * N + (block + 1) * P)
-            c0 = 0
-            for width in widths:
-                cols = slice(c0, c0 + width)
-                if len(widths) > 2 and c0 < 3 * PIECE:
-                    acc = psum.tile([P, BANK], F32, name=f"early{c0}")
+        def product(w, block, spare, first_window=False):
+            window = keep.tile([P, S + spare], F32, name=f"window{w}_{block}")
+            if spare:
+                nc.gpsimd.memset(window[:, S:], 0.0)
+            features = slice(block * P, (block + 1) * P)
+            scale_columns = slice(w * N + block * P, w * N + (block + 1) * P)
+            for first, width in with_starts(FIRST_WINDOW_CUTS if first_window else WINDOW_CUTS):
+                nodes = slice(first, first + width)
+                if width == PIECE:
+                    acc = psum.tile([P, BANK], F32, name=f"own_bank{first}")
                 else:
-                    acc = psum.tile([P, BANK], F32, name="acc", bufs=2)
+                    acc = psum.tile([P, BANK], F32, name="bank_in_turn", bufs=2)
                 nc.tensor.matmul_mx(
                     out=acc[:, :width],
-                    lhsT=w_words[w][:, rows].bitcast(FP8X4),
-                    lhsT_scale=w_scales[:, srows],
-                    rhs=x_words[:, cols].bitcast(FP8X4),
-                    rhs_scale=x_scales[:, cols],
+                    lhsT=w_codes[w][:, features].bitcast(FP8X4),
+                    lhsT_scale=w_scales[:, scale_columns],
+                    rhs=x_codes[:, nodes].bitcast(FP8X4),
+                    rhs_scale=x_scales[:, nodes],
                     start=True,
                     stop=True,
                 )
-                if len(widths) > 2 and c0 + width == S:
-                    nc.vector.tensor_copy(res[:, cols], acc[:, :width])
+                if first_window and first + width == S:
+                    nc.vector.tensor_copy(window[:, nodes], acc[:, :width])
                 else:
-                    nc.scalar.copy(res[:, cols], acc[:, :width])
-                c0 = c0 + width
-            return res
+                    nc.scalar.copy(window[:, nodes], acc[:, :width])
+            return window
 
-        y0 = product(0, 0, (256, 256, 256, 128, 128))
-        e0 = product(1, 0, (BANK, BANK))
-        y1 = product(0, 1, (BANK, BANK))
-        e1 = product(1, 1, (BANK, BANK))
-        h0 = product(2, 0, (BANK, BANK))
-        h1 = product(2, 1, (BANK, BANK))
+        y = [product(0, 0, SPARE_FOR_COPY, first_window=True), product(0, 1, SPARE_FOR_COPY)]
+        e = [product(1, 0, SPARE_FOR_FUSED), product(1, 1, SPARE_FOR_FUSED)]
+        h = [product(2, 0, SPARE_FOR_FUSED), product(2, 1, 0)]
 
-        gates = []
-        for block, (y, e) in enumerate(((y0, e0), (y1, e1))):
-            halves = []
-            for c0 in range(0, U, BANK):
-                at_dst = keep.tile([P, BANK], F32, name=f"at_dst{block}_{c0}")
-                nc.vector.tensor_copy(at_dst[:], y[:].indirect(entries(dst_t, c0, BANK)))
-                halves.append(at_dst)
-            gate = keep.tile([P, U], F32, name=f"gate{block}")
-            for half, c0 in enumerate(range(0, U, BANK)):
-                both = keep.tile([P, BANK], F32, name=f"both{block}_{c0}")
-                nc.vector.tensor_tensor(both[:], e[:].indirect(entries(src_t, c0, BANK)), halves[half][:], ADD)
-                nc.scalar.activation(gate[:, c0 : c0 + BANK], both[:], TANH)
-            gates.append(gate)
+        y_at_dst = []
+        for block in range(N // P):
+            gathered = keep.tile([P, U], F32, name=f"y_at_dst{block}")
+            nc.vector.tensor_copy(gathered[:], y[block][:].indirect(dst_tile[:]))
+            y_at_dst.append(gathered)
 
-        for block, (h, cuts) in enumerate(((h0, (512, 512)), (h1, (512, 256, 128, 128)))):
-            c0 = 0
-            for width in cuts:
-                msg = keep.tile([P, width], F32, name=f"msg{block}_{c0}")
+        gates = keep.tile([P, (N // P) * U], F32, name="gates", tag="codes_then_gates", align_bytes=64)
+        for block in range(N // P):
+            both_ends = keep.tile([P, U], F32, name=f"both_ends{block}")
+            nc.vector.tensor_tensor(both_ends[:], e[block][:].indirect(src_tile[:]), y_at_dst[block][:], ADD)
+            nc.scalar.activation(gates[:, block * U : (block + 1) * U], both_ends[:], TANH)
+
+        for block, cuts in enumerate(OUT_CUTS):
+            for first, width in with_starts(cuts):
+                message = keep.tile([P, width], F32, name=f"message{block}_{first}")
                 nc.vector.tensor_tensor(
-                    msg[:], h[:].indirect(entries(src_t, c0, width)), gates[block][:, c0 : c0 + width], MULT
+                    message[:],
+                    h[block][:].indirect(entries(src_tile, first, width)),
+                    gates[:, block * U + first : block * U + first + width],
+                    MULT,
                 )
-                nc.sync.dma_start(out[block * P : (block + 1) * P, c0 : c0 + width], msg[:])
-                c0 = c0 + width
+                nc.sync.dma_start(out[block * P : (block + 1) * P, first : first + width], message[:])

@@ -15,6 +15,7 @@ FP8X4 = mybir.dt.float8_e4m3fn_x4
 ADD = mybir.AluOpType.add
 MULT = mybir.AluOpType.mult
 TANH = mybir.ActivationFunctionType.Tanh
+COPY = mybir.ActivationFunctionType.Copy
 
 P = 128
 PLANES = 4
@@ -24,12 +25,13 @@ SCALE_ROWS = 4
 BANK = 512
 PIECE = 256
 
-X_LOADS = (
-    ((1024, 0), (512, 512), (512, 192)),
-    ((1024, 704), (512, 0), (256, 256), (256, 80)),
-)
+PAIR_LOADS = ((512, 512), (512, 512), (512, 256), (512, 64))
+LAST_PLANE_LOADS = (256, 512, 512, 512, 256)
+SCALAR_PIECES = ((384, 384), (768, 256))
+VECTOR_PIECES = ((0, 384),)
+PAIR_PIECES = ((0, 1024),)
 
-FIRST_WINDOW_CUTS = (PIECE, PIECE, PIECE, PIECE // 2, PIECE // 2)
+FIRST_WINDOW_CUTS = ((0, 256), (256, 256), (512, 256), (768, 128), (896, 128))
 WINDOW_CUTS = (BANK, BANK)
 
 SPARE_FOR_COPY = 352
@@ -62,16 +64,17 @@ def tile_picked_edgeatt_tanh_e_kernel(
         nc.vector.memset(w_scales[:].bitcast(I32), 0)
 
         x_planes = xT.rearrange("(p j) t -> p j t", j=PLANES)
-        pairs = [keep.tile([P, T], U32, name=f"pairs{u}") for u in range(2)]
-        picked = [keep.tile([P, 2, PIECE], U32, name=f"picked{i}") for i in range(S // PIECE)]
-        x_loaded = []
-        for u, loads in enumerate(X_LOADS):
-            for first, width in with_starts([load[0] for load in loads]):
-                raw = keep.tile([P, 2, width], F32, name=f"raw{u}_{first}")
-                nc.sync.dma_start(raw[:], x_planes[:, 2 * u : 2 * u + 2, first : first + width])
-                x_loaded.append(raw)
-            if u == 0:
-                nc.sync.dma_start(offs_tile[:], offs)
+        plane2 = keep.tile([P, T], F32, name="plane2")
+        nc.sync.dma_start(plane2[:], x_planes[:, 2, :])
+        nc.sync.dma_start(offs_tile[:], offs)
+        pair_loaded = []
+        for first, width in with_starts([load[0] for load in PAIR_LOADS]):
+            raw = keep.tile([P, 2, width], F32, name=f"raw_pair{first}")
+            nc.sync.dma_start(raw[:], x_planes[:, 0:2, first : first + width])
+            pair_loaded.append(raw)
+        plane3 = keep.tile([P, T], F32, name="plane3")
+        for first, width in with_starts(LAST_PLANE_LOADS):
+            nc.sync.dma_start(plane3[:, first : first + width], x_planes[:, 3, first : first + width])
 
         def load_weight(w, words, scales):
             codes = keep.tile([P, N], U32, name=f"w_codes{w}", align_bytes=64)
@@ -90,42 +93,58 @@ def tile_picked_edgeatt_tanh_e_kernel(
         w3_codes = load_weight(2, w3_words, w3_scales)
         w_codes = (w1_codes, w2_codes, w3_codes)
 
-        loads_done = 0
-        for u, loads in enumerate(X_LOADS):
-            first = 0
-            for width, on_scalar in loads:
-                rounded = pairs[u][:, first : first + width].bitcast(BF16).rearrange("p (t e) -> p t e", e=2)
-                by_node = x_loaded[loads_done][:].rearrange("p e t -> p t e")
-                if on_scalar > 0:
-                    nc.scalar.copy(rounded[:, :on_scalar, :], by_node[:, :on_scalar, :])
-                if on_scalar < width:
-                    nc.vector.tensor_copy(rounded[:, on_scalar:, :], by_node[:, on_scalar:, :])
-                first = first + width
-                loads_done = loads_done + 1
-            for i, piece in enumerate(picked):
-                nc.vector.tensor_copy(piece[:, u, :], pairs[u][:].indirect(entries(offs_tile, i * PIECE, PIECE)))
+        woven = keep.tile([P, S * PLANES], BF16, name="woven", align_bytes=64)
+        slots = woven[:].rearrange("p (n j) -> p n j", j=PLANES)
+        word_slots = woven[:].bitcast(U32).rearrange("p (n u) -> p n u", u=2)
+
+        nc.vector.tensor_copy(slots[:, :, 2], plane2[:].indirect(offs_tile[:]))
+
+        pairs = keep.tile([P, T], U32, name="pairs")
+        first = 0
+        for raw, (width, on_scalar) in zip(pair_loaded, PAIR_LOADS):
+            rounded = pairs[:, first : first + width].bitcast(BF16).rearrange("p (t e) -> p t e", e=2)
+            by_node = raw[:].rearrange("p e t -> p t e")
+            if on_scalar > 0:
+                nc.scalar.copy(rounded[:, :on_scalar, :], by_node[:, :on_scalar, :])
+            if on_scalar < width:
+                nc.vector.tensor_copy(rounded[:, on_scalar:, :], by_node[:, on_scalar:, :])
+            first = first + width
+        for first, width in PAIR_PIECES:
+            nc.vector.tensor_copy(
+                word_slots[:, first : first + width, 0], pairs[:].indirect(entries(offs_tile, first, width))
+            )
+
+        first_window = plane2
+        rounded3 = first_window[:, : T // 2].bitcast(BF16)
+        for first, width in with_starts(LAST_PLANE_LOADS):
+            nc.scalar.copy(rounded3[:, first : first + width], plane3[:, first : first + width])
+        for first, width in VECTOR_PIECES:
+            nc.vector.tensor_copy(
+                slots[:, first : first + width, 3], plane3[:].indirect(entries(offs_tile, first, width))
+            )
+        for first, width in SCALAR_PIECES:
+            nc.scalar.activation(
+                slots[:, first : first + width, 3], rounded3.indirect(entries(offs_tile, first, width)), COPY
+            )
 
         x_codes = keep.tile([P, S], U32, name="x_codes", tag="codes_then_gates", align_bytes=64)
         x_scales = keep.tile([P, S], U8, name="x_scales", align_bytes=64)
-        for i, piece in enumerate(picked):
-            woven = keep.tile([P, PIECE, 2], U32, name=f"woven{i}", align_bytes=64)
-            nc.scalar.copy(woven[:], piece[:].rearrange("p u n -> p n u"))
-            for first, width in with_starts(FIRST_WINDOW_CUTS):
-                if first // PIECE == i:
-                    within = first % PIECE
-                    nc.vector.quantize_mx(
-                        out=x_codes[:, first : first + width].bitcast(FP8X4),
-                        scales=x_scales[:, first : first + width],
-                        in_=woven[:, within : within + width, :].rearrange("p n u -> p (n u)").bitcast(BF16),
-                    )
+        for first, width in FIRST_WINDOW_CUTS:
+            nc.vector.quantize_mx(
+                out=x_codes[:, first : first + width].bitcast(FP8X4),
+                scales=x_scales[:, first : first + width],
+                in_=woven[:, first * PLANES : (first + width) * PLANES],
+            )
 
-        def product(w, block, spare, first_window=False):
-            window = keep.tile([P, S + spare], F32, name=f"window{w}_{block}")
-            if spare:
+        def product(w, block, spare, window=None):
+            is_first = window is not None
+            if not is_first:
+                window = keep.tile([P, S + spare], F32, name=f"window{w}_{block}")
+            if spare and not is_first:
                 nc.gpsimd.memset(window[:, S:], 0.0)
             features = slice(block * P, (block + 1) * P)
             scale_columns = slice(w * N + block * P, w * N + (block + 1) * P)
-            for first, width in with_starts(FIRST_WINDOW_CUTS if first_window else WINDOW_CUTS):
+            for first, width in FIRST_WINDOW_CUTS if is_first else with_starts(WINDOW_CUTS):
                 nodes = slice(first, first + width)
                 if width == PIECE:
                     acc = psum.tile([P, BANK], F32, name=f"own_bank{first}")
@@ -140,13 +159,13 @@ def tile_picked_edgeatt_tanh_e_kernel(
                     start=True,
                     stop=True,
                 )
-                if first_window and first + width == S:
+                if is_first and (first, width) == FIRST_WINDOW_CUTS[-1]:
                     nc.vector.tensor_copy(window[:, nodes], acc[:, :width])
                 else:
                     nc.scalar.copy(window[:, nodes], acc[:, :width])
             return window
 
-        y = [product(0, 0, SPARE_FOR_COPY, first_window=True), product(0, 1, SPARE_FOR_COPY)]
+        y = [product(0, 0, SPARE_FOR_COPY, window=first_window), product(0, 1, SPARE_FOR_COPY)]
         e = [product(1, 0, SPARE_FOR_FUSED), product(1, 1, SPARE_FOR_FUSED)]
         h = [product(2, 0, SPARE_FOR_FUSED), product(2, 1, 0)]
 

@@ -25,10 +25,10 @@ SCALE_ROWS = 4
 BANK = 512
 PIECE = 256
 
-PAIR_LOADS = ((512, 512), (512, 512), (512, 256), (512, 64))
-LAST_PLANE_LOADS = (256, 512, 512, 512, 256)
-SCALAR_PIECES = ((384, 384), (768, 256))
-VECTOR_PIECES = ((0, 384),)
+PAIR_LOADS = ((512, 512), (512, 512), (512, 192), (256, 96), (256, 80))
+LAST_PLANE_LOADS = (256, 512, 512, 512, 128, 128)
+SCALAR_PIECES = ((512, 256), (768, 256))
+VECTOR_PIECES = ((0, 512),)
 PAIR_PIECES = ((0, 1024),)
 
 FIRST_WINDOW_CUTS = ((0, 256), (256, 256), (512, 256), (768, 128), (896, 128))
@@ -94,10 +94,10 @@ def tile_picked_edgeatt_tanh_e_kernel(
         w_codes = (w1_codes, w2_codes, w3_codes)
 
         woven = keep.tile([P, S * PLANES], BF16, name="woven", align_bytes=64)
-        slots = woven[:].rearrange("p (n j) -> p n j", j=PLANES)
-        word_slots = woven[:].bitcast(U32).rearrange("p (n u) -> p n u", u=2)
+        picked = keep.tile([P, 2 * S], U32, name="picked")
+        slots = picked[:, S:].bitcast(BF16).rearrange("p (n e) -> p n e", e=2)
 
-        nc.vector.tensor_copy(slots[:, :, 2], plane2[:].indirect(offs_tile[:]))
+        nc.vector.tensor_copy(slots[:, :, 0], plane2[:].indirect(offs_tile[:]))
 
         pairs = keep.tile([P, T], U32, name="pairs")
         first = 0
@@ -111,7 +111,7 @@ def tile_picked_edgeatt_tanh_e_kernel(
             first = first + width
         for first, width in PAIR_PIECES:
             nc.vector.tensor_copy(
-                word_slots[:, first : first + width, 0], pairs[:].indirect(entries(offs_tile, first, width))
+                picked[:, first : first + width], pairs[:].indirect(entries(offs_tile, first, width))
             )
 
         first_window = plane2
@@ -120,12 +120,21 @@ def tile_picked_edgeatt_tanh_e_kernel(
             nc.scalar.copy(rounded3[:, first : first + width], plane3[:, first : first + width])
         for first, width in VECTOR_PIECES:
             nc.vector.tensor_copy(
-                slots[:, first : first + width, 3], plane3[:].indirect(entries(offs_tile, first, width))
+                slots[:, first : first + width, 1], plane3[:].indirect(entries(offs_tile, first, width))
             )
         for first, width in SCALAR_PIECES:
             nc.scalar.activation(
-                slots[:, first : first + width, 3], rounded3.indirect(entries(offs_tile, first, width)), COPY
+                slots[:, first : first + width, 1], rounded3.indirect(entries(offs_tile, first, width)), COPY
             )
+
+        by_pair = picked[:].rearrange("p (u n) -> p n u", u=2)
+        woven_words = woven[:].bitcast(U32).rearrange("p (n u) -> p n u", u=2)
+        for first, width in ((0, 256), (256, 256)):
+            nc.vector.tensor_copy(
+                woven_words[:, first : first + width, :].bitcast(I32), by_pair[:, first : first + width, :].bitcast(I32)
+            )
+        for first, width in ((512, 256), (768, 128), (896, 128)):
+            nc.scalar.copy(woven_words[:, first : first + width, :], by_pair[:, first : first + width, :])
 
         x_codes = keep.tile([P, S], U32, name="x_codes", tag="codes_then_gates", align_bytes=64)
         x_scales = keep.tile([P, S], U8, name="x_scales", align_bytes=64)
@@ -159,7 +168,7 @@ def tile_picked_edgeatt_tanh_e_kernel(
                     start=True,
                     stop=True,
                 )
-                if is_first and (first, width) == FIRST_WINDOW_CUTS[-1]:
+                if is_first and first in (0, 896):
                     nc.vector.tensor_copy(window[:, nodes], acc[:, :width])
                 else:
                     nc.scalar.copy(window[:, nodes], acc[:, :width])

@@ -25,11 +25,11 @@ SCALE_ROWS = 4
 BANK = 512
 PIECE = 256
 
-PAIR_LOADS = ((512, 512), (512, 512), (512, 192), (256, 96), (256, 80))
-LAST_PLANE_LOADS = (256, 512, 512, 512, 128, 128)
+PAIR_LOADS = ((1024, 384), (512, 192), (256, 96), (256, 80))
+PLANE2_LOADS = (512, 512, 512, 512)
+PLANE3_LOADS = ((256, 0), (512, 0), (512, 0), (512, 512), (256, 64))
 SCALAR_PIECES = ((512, 256), (768, 256))
 VECTOR_PIECES = ((0, 512),)
-PAIR_PIECES = ((0, 1024),)
 
 FIRST_WINDOW_CUTS = ((0, 256), (256, 256), (512, 256), (768, 128), (896, 128))
 WINDOW_CUTS = (BANK, BANK)
@@ -64,16 +64,17 @@ def tile_picked_edgeatt_tanh_e_kernel(
         nc.vector.memset(w_scales[:].bitcast(I32), 0)
 
         x_planes = xT.rearrange("(p j) t -> p j t", j=PLANES)
-        plane2 = keep.tile([P, T], F32, name="plane2")
-        nc.sync.dma_start(plane2[:], x_planes[:, 2, :])
-        nc.sync.dma_start(offs_tile[:], offs)
         pair_loaded = []
         for first, width in with_starts([load[0] for load in PAIR_LOADS]):
             raw = keep.tile([P, 2, width], F32, name=f"raw_pair{first}")
             nc.sync.dma_start(raw[:], x_planes[:, 0:2, first : first + width])
             pair_loaded.append(raw)
+        nc.sync.dma_start(offs_tile[:], offs)
+        plane2 = keep.tile([P, T], F32, name="plane2")
+        for first, width in with_starts(PLANE2_LOADS):
+            nc.sync.dma_start(plane2[:, first : first + width], x_planes[:, 2, first : first + width])
         plane3 = keep.tile([P, T], F32, name="plane3")
-        for first, width in with_starts(LAST_PLANE_LOADS):
+        for first, width in with_starts([load[0] for load in PLANE3_LOADS]):
             nc.sync.dma_start(plane3[:, first : first + width], x_planes[:, 3, first : first + width])
 
         def load_weight(w, words, scales):
@@ -97,8 +98,6 @@ def tile_picked_edgeatt_tanh_e_kernel(
         picked = keep.tile([P, 2 * S], U32, name="picked")
         slots = picked[:, S:].bitcast(BF16).rearrange("p (n e) -> p n e", e=2)
 
-        nc.vector.tensor_copy(slots[:, :, 0], plane2[:].indirect(offs_tile[:]))
-
         pairs = keep.tile([P, T], U32, name="pairs")
         first = 0
         for raw, (width, on_scalar) in zip(pair_loaded, PAIR_LOADS):
@@ -109,15 +108,27 @@ def tile_picked_edgeatt_tanh_e_kernel(
             if on_scalar < width:
                 nc.vector.tensor_copy(rounded[:, on_scalar:, :], by_node[:, on_scalar:, :])
             first = first + width
-        for first, width in PAIR_PIECES:
-            nc.vector.tensor_copy(
-                picked[:, first : first + width], pairs[:].indirect(entries(offs_tile, first, width))
-            )
+        nc.vector.tensor_copy(picked[:, :S], pairs[:].indirect(offs_tile[:]))
 
-        first_window = plane2
+        rounded2 = keep.tile([P, T], BF16, name="rounded2")
+        for first, width in with_starts(PLANE2_LOADS):
+            nc.scalar.copy(rounded2[:, first : first + width], plane2[:, first : first + width])
+        first_window = keep.tile([P, S + SPARE_FOR_COPY], F32, name="first_window")
+        nc.gpsimd.memset(first_window[:, S:], 0.0)
         rounded3 = first_window[:, : T // 2].bitcast(BF16)
-        for first, width in with_starts(LAST_PLANE_LOADS):
-            nc.scalar.copy(rounded3[:, first : first + width], plane3[:, first : first + width])
+        for first, width in VECTOR_PIECES:
+            nc.vector.tensor_copy(
+                slots[:, first : first + width, 0], plane2[:].indirect(entries(offs_tile, first, width))
+            )
+        nc.scalar.activation(slots[:, 512:, 0], rounded2[:].indirect(entries(offs_tile, 512, 512)), COPY)
+        first = 0
+        for width, on_scalar in PLANE3_LOADS:
+            cut = first + width - on_scalar
+            if cut > first:
+                nc.gpsimd.tensor_copy(rounded3[:, first:cut], plane3[:, first:cut])
+            if on_scalar > 0:
+                nc.scalar.copy(rounded3[:, cut : first + width], plane3[:, cut : first + width])
+            first = first + width
         for first, width in VECTOR_PIECES:
             nc.vector.tensor_copy(
                 slots[:, first : first + width, 1], plane3[:].indirect(entries(offs_tile, first, width))
@@ -129,11 +140,11 @@ def tile_picked_edgeatt_tanh_e_kernel(
 
         by_pair = picked[:].rearrange("p (u n) -> p n u", u=2)
         woven_words = woven[:].bitcast(U32).rearrange("p (n u) -> p n u", u=2)
-        for first, width in ((0, 256), (256, 256)):
+        for first, width in ((0, 256), (256, 256), (512, 128)):
             nc.vector.tensor_copy(
                 woven_words[:, first : first + width, :].bitcast(I32), by_pair[:, first : first + width, :].bitcast(I32)
             )
-        for first, width in ((512, 256), (768, 128), (896, 128)):
+        for first, width in ((640, 128), (768, 128), (896, 128)):
             nc.scalar.copy(woven_words[:, first : first + width, :], by_pair[:, first : first + width, :])
 
         x_codes = keep.tile([P, S], U32, name="x_codes", tag="codes_then_gates", align_bytes=64)

@@ -26,12 +26,12 @@ BANK = 512
 PIECE = 256
 
 PAIR_LOADS = ((1024, 384), (512, 192), (256, 96), (256, 80))
-PLANE2_LOADS = (512, 512, 512, 512)
-PLANE3_LOADS = ((256, 0), (512, 0), (512, 0), (512, 512), (256, 64))
+PLANE2_LOADS = ((512, 0), (512, 512), (512, 512), (256, 0), (256, 176))
+PLANE3_LOADS = ((256, 0), (512, 0), (512, 64), (512, 512), (256, 96))
 SCALAR_PIECES = ((512, 256), (768, 256))
 VECTOR_PIECES = ((0, 512),)
 
-FIRST_WINDOW_CUTS = ((0, 256), (256, 256), (512, 256), (768, 128), (896, 128))
+FIRST_WINDOW_CUTS = ((256, 256), (0, 256), (512, 256), (768, 128), (896, 128))
 WINDOW_CUTS = (BANK, BANK)
 
 SPARE_FOR_COPY = 352
@@ -71,7 +71,7 @@ def tile_picked_edgeatt_tanh_e_kernel(
             pair_loaded.append(raw)
         nc.sync.dma_start(offs_tile[:], offs)
         plane2 = keep.tile([P, T], F32, name="plane2")
-        for first, width in with_starts(PLANE2_LOADS):
+        for first, width in with_starts([load[0] for load in PLANE2_LOADS]):
             nc.sync.dma_start(plane2[:, first : first + width], x_planes[:, 2, first : first + width])
         plane3 = keep.tile([P, T], F32, name="plane3")
         for first, width in with_starts([load[0] for load in PLANE3_LOADS]):
@@ -111,8 +111,14 @@ def tile_picked_edgeatt_tanh_e_kernel(
         nc.vector.tensor_copy(picked[:, :S], pairs[:].indirect(offs_tile[:]))
 
         rounded2 = keep.tile([P, T], BF16, name="rounded2")
-        for first, width in with_starts(PLANE2_LOADS):
-            nc.scalar.copy(rounded2[:, first : first + width], plane2[:, first : first + width])
+        first = 0
+        for width, on_scalar in PLANE2_LOADS:
+            cut = first + width - on_scalar
+            if cut > first:
+                nc.gpsimd.tensor_copy(rounded2[:, first:cut], plane2[:, first:cut])
+            if on_scalar > 0:
+                nc.scalar.copy(rounded2[:, cut : first + width], plane2[:, cut : first + width])
+            first = first + width
         first_window = keep.tile([P, S + SPARE_FOR_COPY], F32, name="first_window")
         nc.gpsimd.memset(first_window[:, S:], 0.0)
         rounded3 = first_window[:, : T // 2].bitcast(BF16)
@@ -129,7 +135,7 @@ def tile_picked_edgeatt_tanh_e_kernel(
             if on_scalar > 0:
                 nc.scalar.copy(rounded3[:, cut : first + width], plane3[:, cut : first + width])
             first = first + width
-        for first, width in VECTOR_PIECES:
+        for first, width in ((0, 256), (256, 256)):
             nc.vector.tensor_copy(
                 slots[:, first : first + width, 1], plane3[:].indirect(entries(offs_tile, first, width))
             )
@@ -140,7 +146,8 @@ def tile_picked_edgeatt_tanh_e_kernel(
 
         by_pair = picked[:].rearrange("p (u n) -> p n u", u=2)
         woven_words = woven[:].bitcast(U32).rearrange("p (n u) -> p n u", u=2)
-        for first, width in ((0, 256), (256, 256), (512, 128)):
+        nc.gpsimd.tensor_copy(woven_words[:, :256, :], by_pair[:, :256, :])
+        for first, width in ((256, 256), (512, 128)):
             nc.vector.tensor_copy(
                 woven_words[:, first : first + width, :].bitcast(I32), by_pair[:, first : first + width, :].bitcast(I32)
             )
@@ -179,7 +186,7 @@ def tile_picked_edgeatt_tanh_e_kernel(
                     start=True,
                     stop=True,
                 )
-                if is_first and first in (0, 896):
+                if is_first and first in (256, 896):
                     nc.vector.tensor_copy(window[:, nodes], acc[:, :width])
                 else:
                     nc.scalar.copy(window[:, nodes], acc[:, :width])

@@ -23,20 +23,16 @@ ENTRIES_PER_COLUMN = 16
 QUADRANT = 32
 SCALE_ROWS = 4
 BANK = 512
-PIECE = 256
 
-PAIR_LOADS = ((1024, 384), (512, 192), (256, 96), (256, 80))
-PLANE2_LOADS = ((512, 0), (512, 512), (512, 512), (256, 0), (256, 176))
-PLANE3_LOADS = ((256, 0), (512, 0), (512, 64), (512, 512), (256, 96))
-SCALAR_PIECES = ((512, 256), (768, 256))
-VECTOR_PIECES = ((0, 512),)
+PLANE3_LOADS = ((896, 544), (768, 464), (384, 256))
 
-FIRST_WINDOW_CUTS = ((256, 256), (0, 256), (512, 256), (768, 128), (896, 128))
+VECTOR_GATHERS = ((256, 384),)
+SCALAR_GATHERS = ((0, 256), (640, 384))
+VECTOR_WEAVES = ((0, 256), (256, 384))
+SCALAR_WEAVES = ((640, 128), (768, 128), (896, 128))
+FIRST_WINDOW_CUTS = ((0, 256, False), (256, 256, False), (512, 128, False), (640, 128, True), (768, 128, True), (896, 128, True))
 WINDOW_CUTS = (BANK, BANK)
-
-SPARE_FOR_COPY = 352
 SPARE_FOR_FUSED = 16
-
 OUT_CUTS = ((U,), (512, 256, 128, 128))
 
 
@@ -63,16 +59,20 @@ def tile_picked_edgeatt_tanh_e_kernel(
         w_scales = keep.tile([P, 3 * N], U8, name="w_scales", align_bytes=64)
         nc.vector.memset(w_scales[:].bitcast(I32), 0)
 
+        fused_windows = [keep.tile([P, S + SPARE_FOR_FUSED], F32, name=f"fused_window{i}") for i in range(3)]
+        nc.gpsimd.memset(fused_windows[0][:, S:], 0.0)
+        nc.gpsimd.memset(fused_windows[1][:, S:], 0.0)
+        nc.scalar.activation(fused_windows[2][:, S:], fused_windows[0][:, S:], TANH)
+        last_window = keep.tile([P, S], F32, name="last_window")
+
         x_planes = xT.rearrange("(p j) t -> p j t", j=PLANES)
-        pair_loaded = []
-        for first, width in with_starts([load[0] for load in PAIR_LOADS]):
-            raw = keep.tile([P, 2, width], F32, name=f"raw_pair{first}")
-            nc.sync.dma_start(raw[:], x_planes[:, 0:2, first : first + width])
-            pair_loaded.append(raw)
-        nc.sync.dma_start(offs_tile[:], offs)
         plane2 = keep.tile([P, T], F32, name="plane2")
-        for first, width in with_starts([load[0] for load in PLANE2_LOADS]):
-            nc.sync.dma_start(plane2[:, first : first + width], x_planes[:, 2, first : first + width])
+        nc.sync.dma_start(plane2[:], x_planes[:, 2, :])
+        nc.sync.dma_start(offs_tile[:], offs)
+        plane0 = keep.tile([P, T], F32, name="plane0")
+        nc.sync.dma_start(plane0[:], x_planes[:, 0, :])
+        plane1 = keep.tile([P, T], F32, name="plane1")
+        nc.sync.dma_start(plane1[:], x_planes[:, 1, :])
         plane3 = keep.tile([P, T], F32, name="plane3")
         for first, width in with_starts([load[0] for load in PLANE3_LOADS]):
             nc.sync.dma_start(plane3[:, first : first + width], x_planes[:, 3, first : first + width])
@@ -96,84 +96,53 @@ def tile_picked_edgeatt_tanh_e_kernel(
 
         woven = keep.tile([P, S * PLANES], BF16, name="woven", align_bytes=64)
         picked = keep.tile([P, 2 * S], U32, name="picked")
-        slots = picked[:, S:].bitcast(BF16).rearrange("p (n e) -> p n e", e=2)
+        slots = picked[:].bitcast(BF16).rearrange("p (u n e) -> p u n e", u=2, e=2)
 
-        pairs = keep.tile([P, T], U32, name="pairs")
-        first = 0
-        for raw, (width, on_scalar) in zip(pair_loaded, PAIR_LOADS):
-            rounded = pairs[:, first : first + width].bitcast(BF16).rearrange("p (t e) -> p t e", e=2)
-            by_node = raw[:].rearrange("p e t -> p t e")
-            if on_scalar > 0:
-                nc.scalar.copy(rounded[:, :on_scalar, :], by_node[:, :on_scalar, :])
-            if on_scalar < width:
-                nc.vector.tensor_copy(rounded[:, on_scalar:, :], by_node[:, on_scalar:, :])
-            first = first + width
-        nc.vector.tensor_copy(picked[:, :S], pairs[:].indirect(offs_tile[:]))
+        nc.vector.tensor_copy(slots[:, 1, :, 0], plane2[:].indirect(offs_tile[:]))
+        nc.vector.tensor_copy(slots[:, 0, :, 0], plane0[:].indirect(offs_tile[:]))
+        nc.vector.tensor_copy(slots[:, 0, :, 1], plane1[:].indirect(offs_tile[:]))
 
-        rounded2 = keep.tile([P, T], BF16, name="rounded2")
-        first = 0
-        for width, on_scalar in PLANE2_LOADS:
-            cut = first + width - on_scalar
-            if cut > first:
-                nc.gpsimd.tensor_copy(rounded2[:, first:cut], plane2[:, first:cut])
-            if on_scalar > 0:
-                nc.scalar.copy(rounded2[:, cut : first + width], plane2[:, cut : first + width])
-            first = first + width
-        first_window = keep.tile([P, S + SPARE_FOR_COPY], F32, name="first_window")
-        nc.gpsimd.memset(first_window[:, S:], 0.0)
-        rounded3 = first_window[:, : T // 2].bitcast(BF16)
-        for first, width in VECTOR_PIECES:
-            nc.vector.tensor_copy(
-                slots[:, first : first + width, 0], plane2[:].indirect(entries(offs_tile, first, width))
-            )
-        nc.scalar.activation(slots[:, 512:, 0], rounded2[:].indirect(entries(offs_tile, 512, 512)), COPY)
+        rounded3 = plane2[:, : T // 2].bitcast(BF16)
         first = 0
         for width, on_scalar in PLANE3_LOADS:
-            cut = first + width - on_scalar
-            if cut > first:
-                nc.gpsimd.tensor_copy(rounded3[:, first:cut], plane3[:, first:cut])
-            if on_scalar > 0:
-                nc.scalar.copy(rounded3[:, cut : first + width], plane3[:, cut : first + width])
+            cut = first + on_scalar
+            nc.scalar.copy(rounded3[:, first:cut], plane3[:, first:cut])
+            nc.gpsimd.tensor_copy(rounded3[:, cut : first + width], plane3[:, cut : first + width])
             first = first + width
-        for first, width in ((0, 256), (256, 256)):
+        for first, width in VECTOR_GATHERS:
             nc.vector.tensor_copy(
-                slots[:, first : first + width, 1], plane3[:].indirect(entries(offs_tile, first, width))
+                slots[:, 1, first : first + width, 1], plane3[:].indirect(entries(offs_tile, first, width))
             )
-        for first, width in SCALAR_PIECES:
+        for first, width in SCALAR_GATHERS:
             nc.scalar.activation(
-                slots[:, first : first + width, 1], rounded3.indirect(entries(offs_tile, first, width)), COPY
+                slots[:, 1, first : first + width, 1], rounded3.indirect(entries(offs_tile, first, width)), COPY
             )
 
         by_pair = picked[:].rearrange("p (u n) -> p n u", u=2)
         woven_words = woven[:].bitcast(U32).rearrange("p (n u) -> p n u", u=2)
-        nc.gpsimd.tensor_copy(woven_words[:, :256, :], by_pair[:, :256, :])
-        for first, width in ((256, 256), (512, 128)):
+        for first, width in VECTOR_WEAVES:
             nc.vector.tensor_copy(
                 woven_words[:, first : first + width, :].bitcast(I32), by_pair[:, first : first + width, :].bitcast(I32)
             )
-        for first, width in ((640, 128), (768, 128), (896, 128)):
+        for first, width in SCALAR_WEAVES:
             nc.scalar.copy(woven_words[:, first : first + width, :], by_pair[:, first : first + width, :])
 
         x_codes = keep.tile([P, S], U32, name="x_codes", tag="codes_then_gates", align_bytes=64)
         x_scales = keep.tile([P, S], U8, name="x_scales", align_bytes=64)
-        for first, width in FIRST_WINDOW_CUTS:
+        for first, width, on_vector in FIRST_WINDOW_CUTS:
             nc.vector.quantize_mx(
                 out=x_codes[:, first : first + width].bitcast(FP8X4),
                 scales=x_scales[:, first : first + width],
                 in_=woven[:, first * PLANES : (first + width) * PLANES],
             )
 
-        def product(w, block, spare, window=None):
-            is_first = window is not None
-            if not is_first:
-                window = keep.tile([P, S + spare], F32, name=f"window{w}_{block}")
-            if spare and not is_first:
-                nc.gpsimd.memset(window[:, S:], 0.0)
+        def product(w, block, window, is_first=False):
             features = slice(block * P, (block + 1) * P)
             scale_columns = slice(w * N + block * P, w * N + (block + 1) * P)
-            for first, width in FIRST_WINDOW_CUTS if is_first else with_starts(WINDOW_CUTS):
+            cuts = FIRST_WINDOW_CUTS if is_first else [cut + (False,) for cut in with_starts(WINDOW_CUTS)]
+            for first, width, on_vector in cuts:
                 nodes = slice(first, first + width)
-                if width == PIECE:
+                if is_first:
                     acc = psum.tile([P, BANK], F32, name=f"own_bank{first}")
                 else:
                     acc = psum.tile([P, BANK], F32, name="bank_in_turn", bufs=2)
@@ -186,15 +155,15 @@ def tile_picked_edgeatt_tanh_e_kernel(
                     start=True,
                     stop=True,
                 )
-                if is_first and first in (256, 896):
+                if on_vector:
                     nc.vector.tensor_copy(window[:, nodes], acc[:, :width])
                 else:
                     nc.scalar.copy(window[:, nodes], acc[:, :width])
             return window
 
-        y = [product(0, 0, SPARE_FOR_COPY, window=first_window), product(0, 1, SPARE_FOR_COPY)]
-        e = [product(1, 0, SPARE_FOR_FUSED), product(1, 1, SPARE_FOR_FUSED)]
-        h = [product(2, 0, SPARE_FOR_FUSED), product(2, 1, 0)]
+        y = [product(0, 0, plane2, is_first=True), product(0, 1, plane3)]
+        e = [product(1, 0, fused_windows[0]), product(1, 1, fused_windows[1])]
+        h = [product(2, 0, fused_windows[2]), product(2, 1, last_window)]
 
         y_at_dst = []
         for block in range(N // P):

@@ -24,13 +24,14 @@ QUADRANT = 32
 SCALE_ROWS = 4
 BANK = 512
 
+PLANE2_ROUNDED_ON_SCALAR = 1216
 PLANE3_LOADS = ((896, 544), (768, 464), (384, 256))
 
-VECTOR_GATHERS = ((256, 384),)
-SCALAR_GATHERS = ((0, 256), (640, 384))
-VECTOR_WEAVES = ((0, 256), (256, 384))
-SCALAR_WEAVES = ((640, 128), (768, 128), (896, 128))
-FIRST_WINDOW_CUTS = ((0, 256, False), (256, 256, False), (512, 128, False), (640, 128, True), (768, 128, True), (896, 128, True))
+VECTOR_GATHERS = ((0, 256), (256, 256))
+SCALAR_GATHERS = ((512, 256), (768, 256))
+VECTOR_WEAVES = ((0, 256), (256, 256))
+SCALAR_WEAVES = ((512, 256), (768, 128), (896, 128))
+FIRST_WINDOW_CUTS = ((0, 256, False), (256, 256, False), (512, 256, False), (768, 128, True), (896, 128, True))
 WINDOW_CUTS = (BANK, BANK)
 SPARE_FOR_FUSED = 16
 OUT_CUTS = ((U,), (512, 256, 128, 128))
@@ -66,11 +67,11 @@ def tile_picked_edgeatt_tanh_e_kernel(
         last_window = keep.tile([P, S], F32, name="last_window")
 
         x_planes = xT.rearrange("(p j) t -> p j t", j=PLANES)
-        plane2 = keep.tile([P, T], F32, name="plane2")
-        nc.sync.dma_start(plane2[:], x_planes[:, 2, :])
-        nc.sync.dma_start(offs_tile[:], offs)
         plane0 = keep.tile([P, T], F32, name="plane0")
         nc.sync.dma_start(plane0[:], x_planes[:, 0, :])
+        nc.sync.dma_start(offs_tile[:], offs)
+        plane2 = keep.tile([P, T], F32, name="plane2")
+        nc.sync.dma_start(plane2[:], x_planes[:, 2, :])
         plane1 = keep.tile([P, T], F32, name="plane1")
         nc.sync.dma_start(plane1[:], x_planes[:, 1, :])
         plane3 = keep.tile([P, T], F32, name="plane3")
@@ -98,11 +99,16 @@ def tile_picked_edgeatt_tanh_e_kernel(
         picked = keep.tile([P, 2 * S], U32, name="picked")
         slots = picked[:].bitcast(BF16).rearrange("p (u n e) -> p u n e", u=2, e=2)
 
-        nc.vector.tensor_copy(slots[:, 1, :, 0], plane2[:].indirect(offs_tile[:]))
         nc.vector.tensor_copy(slots[:, 0, :, 0], plane0[:].indirect(offs_tile[:]))
+        rounded2 = keep.tile([P, T], BF16, name="rounded2")
+        cut = PLANE2_ROUNDED_ON_SCALAR
+        nc.scalar.copy(rounded2[:, :cut], plane2[:, :cut])
+        nc.gpsimd.tensor_copy(rounded2[:, cut:], plane2[:, cut:])
+        nc.vector.tensor_copy(slots[:, 1, : S // 2, 0], plane2[:].indirect(entries(offs_tile, 0, S // 2)))
+        nc.scalar.activation(slots[:, 1, S // 2 :, 0], rounded2[:].indirect(entries(offs_tile, S // 2, S // 2)), COPY)
         nc.vector.tensor_copy(slots[:, 0, :, 1], plane1[:].indirect(offs_tile[:]))
 
-        rounded3 = plane2[:, : T // 2].bitcast(BF16)
+        rounded3 = plane0[:, : T // 2].bitcast(BF16)
         first = 0
         for width, on_scalar in PLANE3_LOADS:
             cut = first + on_scalar
@@ -161,7 +167,7 @@ def tile_picked_edgeatt_tanh_e_kernel(
                     nc.scalar.copy(window[:, nodes], acc[:, :width])
             return window
 
-        y = [product(0, 0, plane2, is_first=True), product(0, 1, plane3)]
+        y = [product(0, 0, plane0, is_first=True), product(0, 1, plane3)]
         e = [product(1, 0, fused_windows[0]), product(1, 1, fused_windows[1])]
         h = [product(2, 0, fused_windows[2]), product(2, 1, last_window)]
 

@@ -25,13 +25,14 @@ SCALE_ROWS = 4
 BANK = 512
 
 PLANE2_ROUNDED_ON_SCALAR = 1216
-PLANE3_LOADS = ((896, 544), (768, 464), (384, 256))
+PLANE3_LOADS = ((1024, 608), (640, 384), (384, 240))
 
 VECTOR_GATHERS = ((0, 256), (256, 256))
 SCALAR_GATHERS = ((512, 256), (768, 256))
 VECTOR_WEAVES = ((0, 256), (256, 256))
-SCALAR_WEAVES = ((512, 256), (768, 128), (896, 128))
-FIRST_WINDOW_CUTS = ((0, 256, False), (256, 256, False), (512, 256, False), (768, 128, True), (896, 128, True))
+SCALAR_WEAVES = ((512, 128), (640, 128), (768, 128), (896, 64), (960, 64))
+FIRST_WINDOW_CUTS = ((0, 256, False), (256, 256, False), (512, 256, False), (768, 128, True), (896, 64, True), (960, 64, True))
+QUANTISE_CUTS = ((0, 256), (256, 256), (512, 128), (640, 128), (768, 128), (896, 64), (960, 64))
 WINDOW_CUTS = (BANK, BANK)
 SPARE_FOR_FUSED = 16
 OUT_CUTS = ((U,), (512, 256, 128, 128))
@@ -128,14 +129,15 @@ def tile_picked_edgeatt_tanh_e_kernel(
         woven_words = woven[:].bitcast(U32).rearrange("p (n u) -> p n u", u=2)
         for first, width in VECTOR_WEAVES:
             nc.vector.tensor_copy(
-                woven_words[:, first : first + width, :].bitcast(I32), by_pair[:, first : first + width, :].bitcast(I32)
+                woven_words[:, first : first + width, :].bitcast(I32).rearrange("p (c i) u -> p c u i", i=4),
+                by_pair[:, first : first + width, :].bitcast(I32).rearrange("p (c i) u -> p c u i", i=4),
             )
         for first, width in SCALAR_WEAVES:
             nc.scalar.copy(woven_words[:, first : first + width, :], by_pair[:, first : first + width, :])
 
         x_codes = keep.tile([P, S], U32, name="x_codes", tag="codes_then_gates", align_bytes=64)
         x_scales = keep.tile([P, S], U8, name="x_scales", align_bytes=64)
-        for first, width, on_vector in FIRST_WINDOW_CUTS:
+        for first, width in QUANTISE_CUTS:
             nc.vector.quantize_mx(
                 out=x_codes[:, first : first + width].bitcast(FP8X4),
                 scales=x_scales[:, first : first + width],
@@ -148,7 +150,7 @@ def tile_picked_edgeatt_tanh_e_kernel(
             cuts = FIRST_WINDOW_CUTS if is_first else [cut + (False,) for cut in with_starts(WINDOW_CUTS)]
             for first, width, on_vector in cuts:
                 nodes = slice(first, first + width)
-                if is_first:
+                if is_first and width > 64:
                     acc = psum.tile([P, BANK], F32, name=f"own_bank{first}")
                 else:
                     acc = psum.tile([P, BANK], F32, name="bank_in_turn", bufs=2)

@@ -150,10 +150,10 @@ def tile_picked_edgeatt_tanh_e_kernel(
             cuts = FIRST_WINDOW_CUTS if is_first else [cut + (False,) for cut in with_starts(WINDOW_CUTS)]
             for first, width, on_vector in cuts:
                 nodes = slice(first, first + width)
-                if is_first and width > 64:
+                if is_first and first < S // 2:
                     acc = psum.tile([P, BANK], F32, name=f"own_bank{first}")
                 else:
-                    acc = psum.tile([P, BANK], F32, name="bank_in_turn", bufs=2)
+                    acc = psum.tile([P, BANK], F32, name="bank_in_turn", bufs=4)
                 nc.tensor.matmul_mx(
                     out=acc[:, :width],
                     lhsT=w_codes[w][:, features].bitcast(FP8X4),

@@ -23,19 +23,31 @@ ENTRIES_PER_COLUMN = 16
 QUADRANT = 32
 SCALE_ROWS = 4
 BANK = 512
+BANKS_IN_TURN = 4
+HALF = S // 2
+WORDS_PER_LINE = 4
 
 PLANE2_ROUNDED_ON_SCALAR = 1216
 PLANE3_LOADS = ((1024, 608), (640, 384), (384, 240))
 
 VECTOR_GATHERS = ((0, 256), (256, 256))
 SCALAR_GATHERS = ((512, 256), (768, 256))
-VECTOR_WEAVES = ((0, 256), (256, 256))
+VECTOR_WEAVES = VECTOR_GATHERS
 SCALAR_WEAVES = ((512, 128), (640, 128), (768, 128), (896, 64), (960, 64))
-FIRST_WINDOW_CUTS = ((0, 256, False), (256, 256, False), (512, 256, False), (768, 128, True), (896, 64, True), (960, 64, True))
-QUANTISE_CUTS = ((0, 256), (256, 256), (512, 128), (640, 128), (768, 128), (896, 64), (960, 64))
-WINDOW_CUTS = (BANK, BANK)
-SPARE_FOR_FUSED = 16
-OUT_CUTS = ((U,), (512, 256, 128, 128))
+QUANTISE_CUTS = VECTOR_WEAVES + SCALAR_WEAVES
+FIRST_PRODUCT_CUTS = (
+    (0, 256, False),
+    (256, 256, False),
+    (512, 256, False),
+    (768, 128, True),
+    (896, 64, True),
+    (960, 64, True),
+)
+LATER_PRODUCT_CUTS = ((0, BANK, False), (BANK, BANK, False))
+
+SPARE_COLUMNS = 16
+
+OUT_CUTS = ((512, 512), (512, 256, 128, 128))
 
 
 def entries(list_tile, first, count):
@@ -61,7 +73,7 @@ def tile_picked_edgeatt_tanh_e_kernel(
         w_scales = keep.tile([P, 3 * N], U8, name="w_scales", align_bytes=64)
         nc.vector.memset(w_scales[:].bitcast(I32), 0)
 
-        fused_windows = [keep.tile([P, S + SPARE_FOR_FUSED], F32, name=f"fused_window{i}") for i in range(3)]
+        fused_windows = [keep.tile([P, S + SPARE_COLUMNS], F32, name=f"fused_window{i}") for i in range(3)]
         nc.gpsimd.memset(fused_windows[0][:, S:], 0.0)
         nc.gpsimd.memset(fused_windows[1][:, S:], 0.0)
         nc.scalar.activation(fused_windows[2][:, S:], fused_windows[0][:, S:], TANH)
@@ -98,16 +110,16 @@ def tile_picked_edgeatt_tanh_e_kernel(
 
         woven = keep.tile([P, S * PLANES], BF16, name="woven", align_bytes=64)
         picked = keep.tile([P, 2 * S], U32, name="picked")
-        slots = picked[:].bitcast(BF16).rearrange("p (u n e) -> p u n e", u=2, e=2)
+        halves = picked[:].bitcast(BF16).rearrange("p (u n e) -> p u n e", u=2, e=2)
 
-        nc.vector.tensor_copy(slots[:, 0, :, 0], plane0[:].indirect(offs_tile[:]))
+        nc.vector.tensor_copy(halves[:, 0, :, 0], plane0[:].indirect(offs_tile[:]))
         rounded2 = keep.tile([P, T], BF16, name="rounded2")
         cut = PLANE2_ROUNDED_ON_SCALAR
         nc.scalar.copy(rounded2[:, :cut], plane2[:, :cut])
         nc.gpsimd.tensor_copy(rounded2[:, cut:], plane2[:, cut:])
-        nc.vector.tensor_copy(slots[:, 1, : S // 2, 0], plane2[:].indirect(entries(offs_tile, 0, S // 2)))
-        nc.scalar.activation(slots[:, 1, S // 2 :, 0], rounded2[:].indirect(entries(offs_tile, S // 2, S // 2)), COPY)
-        nc.vector.tensor_copy(slots[:, 0, :, 1], plane1[:].indirect(offs_tile[:]))
+        nc.vector.tensor_copy(halves[:, 1, :HALF, 0], plane2[:].indirect(entries(offs_tile, 0, HALF)))
+        nc.scalar.activation(halves[:, 1, HALF:, 0], rounded2[:].indirect(entries(offs_tile, HALF, HALF)), COPY)
+        nc.vector.tensor_copy(halves[:, 0, :, 1], plane1[:].indirect(offs_tile[:]))
 
         rounded3 = plane0[:, : T // 2].bitcast(BF16)
         first = 0
@@ -118,19 +130,19 @@ def tile_picked_edgeatt_tanh_e_kernel(
             first = first + width
         for first, width in VECTOR_GATHERS:
             nc.vector.tensor_copy(
-                slots[:, 1, first : first + width, 1], plane3[:].indirect(entries(offs_tile, first, width))
+                halves[:, 1, first : first + width, 1], plane3[:].indirect(entries(offs_tile, first, width))
             )
         for first, width in SCALAR_GATHERS:
             nc.scalar.activation(
-                slots[:, 1, first : first + width, 1], rounded3.indirect(entries(offs_tile, first, width)), COPY
+                halves[:, 1, first : first + width, 1], rounded3.indirect(entries(offs_tile, first, width)), COPY
             )
 
         by_pair = picked[:].rearrange("p (u n) -> p n u", u=2)
         woven_words = woven[:].bitcast(U32).rearrange("p (n u) -> p n u", u=2)
         for first, width in VECTOR_WEAVES:
             nc.vector.tensor_copy(
-                woven_words[:, first : first + width, :].bitcast(I32).rearrange("p (c i) u -> p c u i", i=4),
-                by_pair[:, first : first + width, :].bitcast(I32).rearrange("p (c i) u -> p c u i", i=4),
+                woven_words[:, first : first + width, :].bitcast(I32).rearrange("p (c i) u -> p c u i", i=WORDS_PER_LINE),
+                by_pair[:, first : first + width, :].bitcast(I32).rearrange("p (c i) u -> p c u i", i=WORDS_PER_LINE),
             )
         for first, width in SCALAR_WEAVES:
             nc.scalar.copy(woven_words[:, first : first + width, :], by_pair[:, first : first + width, :])
@@ -144,16 +156,15 @@ def tile_picked_edgeatt_tanh_e_kernel(
                 in_=woven[:, first * PLANES : (first + width) * PLANES],
             )
 
-        def product(w, block, window, is_first=False):
+        def product(w, block, window, cuts):
             features = slice(block * P, (block + 1) * P)
             scale_columns = slice(w * N + block * P, w * N + (block + 1) * P)
-            cuts = FIRST_WINDOW_CUTS if is_first else [cut + (False,) for cut in with_starts(WINDOW_CUTS)]
             for first, width, on_vector in cuts:
                 nodes = slice(first, first + width)
-                if is_first and first < S // 2:
+                if first + width <= HALF and width < BANK:
                     acc = psum.tile([P, BANK], F32, name=f"own_bank{first}")
                 else:
-                    acc = psum.tile([P, BANK], F32, name="bank_in_turn", bufs=4)
+                    acc = psum.tile([P, BANK], F32, name="bank_in_turn", bufs=BANKS_IN_TURN)
                 nc.tensor.matmul_mx(
                     out=acc[:, :width],
                     lhsT=w_codes[w][:, features].bitcast(FP8X4),
@@ -169,9 +180,9 @@ def tile_picked_edgeatt_tanh_e_kernel(
                     nc.scalar.copy(window[:, nodes], acc[:, :width])
             return window
 
-        y = [product(0, 0, plane0, is_first=True), product(0, 1, plane3)]
-        e = [product(1, 0, fused_windows[0]), product(1, 1, fused_windows[1])]
-        h = [product(2, 0, fused_windows[2]), product(2, 1, last_window)]
+        y = [product(0, 0, plane0, FIRST_PRODUCT_CUTS), product(0, 1, plane3, LATER_PRODUCT_CUTS)]
+        e = [product(1, 0, fused_windows[0], LATER_PRODUCT_CUTS), product(1, 1, fused_windows[1], LATER_PRODUCT_CUTS)]
+        h = [product(2, 0, fused_windows[2], LATER_PRODUCT_CUTS), product(2, 1, last_window, LATER_PRODUCT_CUTS)]
 
         y_at_dst = []
         for block in range(N // P):

@@ -47,7 +47,7 @@ LATER_PRODUCT_CUTS = ((0, BANK, False), (BANK, BANK, False))
 
 SPARE_COLUMNS = 16
 
-OUT_CUTS = ((512, 512), (512, 256, 128, 128))
+OUT_CUTS = ((512, 512), (416, 288, 192, 128))
 
 
 def entries(list_tile, first, count):

@@ -73,11 +73,10 @@ def tile_picked_edgeatt_tanh_e_kernel(
         w_scales = keep.tile([P, 3 * N], U8, name="w_scales", align_bytes=64)
         nc.vector.memset(w_scales[:].bitcast(I32), 0)
 
-        fused_windows = [keep.tile([P, S + SPARE_COLUMNS], F32, name=f"fused_window{i}") for i in range(3)]
-        nc.gpsimd.memset(fused_windows[0][:, S:], 0.0)
-        nc.gpsimd.memset(fused_windows[1][:, S:], 0.0)
-        nc.scalar.activation(fused_windows[2][:, S:], fused_windows[0][:, S:], TANH)
-        last_window = keep.tile([P, S], F32, name="last_window")
+        e_windows = [keep.tile([P, S + SPARE_COLUMNS], F32, name=f"e_window{block}") for block in range(N // P)]
+        for window in e_windows:
+            nc.gpsimd.memset(window[:, S:], 0.0)
+        h_windows = [keep.tile([P, S], F32, name=f"h_window{block}") for block in range(N // P)]
 
         x_planes = xT.rearrange("(p j) t -> p j t", j=PLANES)
         plane0 = keep.tile([P, T], F32, name="plane0")
@@ -161,7 +160,7 @@ def tile_picked_edgeatt_tanh_e_kernel(
             scale_columns = slice(w * N + block * P, w * N + (block + 1) * P)
             for first, width, on_vector in cuts:
                 nodes = slice(first, first + width)
-                if first + width <= HALF and width < BANK:
+                if cuts == FIRST_PRODUCT_CUTS and first < HALF:
                     acc = psum.tile([P, BANK], F32, name=f"own_bank{first}")
                 else:
                     acc = psum.tile([P, BANK], F32, name="bank_in_turn", bufs=BANKS_IN_TURN)
@@ -181,8 +180,8 @@ def tile_picked_edgeatt_tanh_e_kernel(
             return window
 
         y = [product(0, 0, plane0, FIRST_PRODUCT_CUTS), product(0, 1, plane3, LATER_PRODUCT_CUTS)]
-        e = [product(1, 0, fused_windows[0], LATER_PRODUCT_CUTS), product(1, 1, fused_windows[1], LATER_PRODUCT_CUTS)]
-        h = [product(2, 0, fused_windows[2], LATER_PRODUCT_CUTS), product(2, 1, last_window, LATER_PRODUCT_CUTS)]
+        e = [product(1, block, e_windows[block], LATER_PRODUCT_CUTS) for block in range(N // P)]
+        h = [product(2, block, h_windows[block], LATER_PRODUCT_CUTS) for block in range(N // P)]
 
         y_at_dst = []
         for block in range(N // P):

@@ -23,31 +23,10 @@ ENTRIES_PER_COLUMN = 16
 QUADRANT = 32
 SCALE_ROWS = 4
 BANK = 512
-BANKS_IN_TURN = 4
-HALF = S // 2
-WORDS_PER_LINE = 4
+BANKS = 8
 
-PLANE2_ROUNDED_ON_SCALAR = 1216
-PLANE3_LOADS = ((1024, 608), (640, 384), (384, 240))
-
-VECTOR_GATHERS = ((0, 256), (256, 256))
-SCALAR_GATHERS = ((512, 256), (768, 256))
-VECTOR_WEAVES = VECTOR_GATHERS
-SCALAR_WEAVES = ((512, 128), (640, 128), (768, 128), (896, 64), (960, 64))
-QUANTISE_CUTS = VECTOR_WEAVES + SCALAR_WEAVES
-FIRST_PRODUCT_CUTS = (
-    (0, 256, False),
-    (256, 256, False),
-    (512, 256, False),
-    (768, 128, True),
-    (896, 64, True),
-    (960, 64, True),
-)
-LATER_PRODUCT_CUTS = ((0, BANK, False), (BANK, BANK, False))
-
-SPARE_COLUMNS = 16
-
-OUT_CUTS = ((512, 512), (416, 288, 192, 128))
+SCALAR_SHARE = 256
+CUT = 256
 
 
 def entries(list_tile, first, count):
@@ -73,22 +52,12 @@ def tile_picked_edgeatt_tanh_e_kernel(
         w_scales = keep.tile([P, 3 * N], U8, name="w_scales", align_bytes=64)
         nc.vector.memset(w_scales[:].bitcast(I32), 0)
 
-        e_windows = [keep.tile([P, S + SPARE_COLUMNS], F32, name=f"e_window{block}") for block in range(N // P)]
-        for window in e_windows:
-            nc.gpsimd.memset(window[:, S:], 0.0)
-        h_windows = [keep.tile([P, S], F32, name=f"h_window{block}") for block in range(N // P)]
-
         x_planes = xT.rearrange("(p j) t -> p j t", j=PLANES)
-        plane0 = keep.tile([P, T], F32, name="plane0")
-        nc.sync.dma_start(plane0[:], x_planes[:, 0, :])
+        planes = [keep.tile([P, T], F32, name=f"plane{j}") for j in range(PLANES)]
+        nc.sync.dma_start(planes[2][:], x_planes[:, 2, :])
         nc.sync.dma_start(offs_tile[:], offs)
-        plane2 = keep.tile([P, T], F32, name="plane2")
-        nc.sync.dma_start(plane2[:], x_planes[:, 2, :])
-        plane1 = keep.tile([P, T], F32, name="plane1")
-        nc.sync.dma_start(plane1[:], x_planes[:, 1, :])
-        plane3 = keep.tile([P, T], F32, name="plane3")
-        for first, width in with_starts([load[0] for load in PLANE3_LOADS]):
-            nc.sync.dma_start(plane3[:, first : first + width], x_planes[:, 3, first : first + width])
+        for j in (0, 1, 3):
+            nc.sync.dma_start(planes[j][:], x_planes[:, j, :])
 
         def load_weight(w, words, scales):
             codes = keep.tile([P, N], U32, name=f"w_codes{w}", align_bytes=64)
@@ -101,107 +70,151 @@ def tile_picked_edgeatt_tanh_e_kernel(
             return codes
 
         w1_codes = load_weight(0, w1_words, w1_scales)
-        nc.sync.dma_start(dst_tile[:], dst)
         w2_codes = load_weight(1, w2_words, w2_scales)
-        nc.sync.dma_start(src_tile[:], src)
+        nc.sync.dma_start(dst_tile[:], dst)
         w3_codes = load_weight(2, w3_words, w3_scales)
+        nc.sync.dma_start(src_tile[:], src)
         w_codes = (w1_codes, w2_codes, w3_codes)
 
         woven = keep.tile([P, S * PLANES], BF16, name="woven", align_bytes=64)
         picked = keep.tile([P, 2 * S], U32, name="picked")
         halves = picked[:].bitcast(BF16).rearrange("p (u n e) -> p u n e", u=2, e=2)
+        own = S - SCALAR_SHARE
+        apart = keep.tile([P, 2, SCALAR_SHARE], BF16, name="apart")
 
-        nc.vector.tensor_copy(halves[:, 0, :, 0], plane0[:].indirect(offs_tile[:]))
-        rounded2 = keep.tile([P, T], BF16, name="rounded2")
-        cut = PLANE2_ROUNDED_ON_SCALAR
-        nc.scalar.copy(rounded2[:, :cut], plane2[:, :cut])
-        nc.gpsimd.tensor_copy(rounded2[:, cut:], plane2[:, cut:])
-        nc.vector.tensor_copy(halves[:, 1, :HALF, 0], plane2[:].indirect(entries(offs_tile, 0, HALF)))
-        nc.scalar.activation(halves[:, 1, HALF:, 0], rounded2[:].indirect(entries(offs_tile, HALF, HALF)), COPY)
-        nc.vector.tensor_copy(halves[:, 0, :, 1], plane1[:].indirect(offs_tile[:]))
-
-        rounded3 = plane0[:, : T // 2].bitcast(BF16)
-        first = 0
-        for width, on_scalar in PLANE3_LOADS:
-            cut = first + on_scalar
-            nc.scalar.copy(rounded3[:, first:cut], plane3[:, first:cut])
-            nc.gpsimd.tensor_copy(rounded3[:, cut : first + width], plane3[:, cut : first + width])
-            first = first + width
-        for first, width in VECTOR_GATHERS:
-            nc.vector.tensor_copy(
-                halves[:, 1, first : first + width, 1], plane3[:].indirect(entries(offs_tile, first, width))
-            )
-        for first, width in SCALAR_GATHERS:
-            nc.scalar.activation(
-                halves[:, 1, first : first + width, 1], rounded3.indirect(entries(offs_tile, first, width)), COPY
-            )
+        nc.vector.tensor_copy(halves[:, 1, :, 0], planes[2][:].indirect(offs_tile[:]))
+        for j in (0, 1):
+            nc.vector.tensor_copy(halves[:, 0, :own, j], planes[j][:].indirect(entries(offs_tile, 0, own)))
+            nc.scalar.activation(apart[:, j, :], planes[j][:].indirect(entries(offs_tile, own, SCALAR_SHARE)), COPY)
+        nc.scalar.copy(halves[:, 0, own:, :], apart[:].rearrange("p e n -> p n e"))
 
         by_pair = picked[:].rearrange("p (u n) -> p n u", u=2)
         woven_words = woven[:].bitcast(U32).rearrange("p (n u) -> p n u", u=2)
-        for first, width in VECTOR_WEAVES:
+        x_codes = keep.tile([P, S], U32, name="x_codes", align_bytes=64)
+        x_scales = keep.tile([P, S], U8, name="x_scales", align_bytes=64)
+
+        def gather_last(first, width):
             nc.vector.tensor_copy(
-                woven_words[:, first : first + width, :].bitcast(I32).rearrange("p (c i) u -> p c u i", i=WORDS_PER_LINE),
-                by_pair[:, first : first + width, :].bitcast(I32).rearrange("p (c i) u -> p c u i", i=WORDS_PER_LINE),
+                halves[:, 1, first : first + width, 1], planes[3][:].indirect(entries(offs_tile, first, width))
             )
-        for first, width in SCALAR_WEAVES:
+
+        def weave(first, width):
             nc.scalar.copy(woven_words[:, first : first + width, :], by_pair[:, first : first + width, :])
 
-        x_codes = keep.tile([P, S], U32, name="x_codes", tag="codes_then_gates", align_bytes=64)
-        x_scales = keep.tile([P, S], U8, name="x_scales", align_bytes=64)
-        for first, width in QUANTISE_CUTS:
+        def quantise(first, width):
             nc.vector.quantize_mx(
                 out=x_codes[:, first : first + width].bitcast(FP8X4),
                 scales=x_scales[:, first : first + width],
                 in_=woven[:, first * PLANES : (first + width) * PLANES],
             )
 
-        def product(w, block, window, cuts):
-            features = slice(block * P, (block + 1) * P)
-            scale_columns = slice(w * N + block * P, w * N + (block + 1) * P)
-            for first, width, on_vector in cuts:
-                nodes = slice(first, first + width)
-                if cuts == FIRST_PRODUCT_CUTS and first < HALF:
-                    acc = psum.tile([P, BANK], F32, name=f"own_bank{first}")
-                else:
-                    acc = psum.tile([P, BANK], F32, name="bank_in_turn", bufs=BANKS_IN_TURN)
-                nc.tensor.matmul_mx(
-                    out=acc[:, :width],
-                    lhsT=w_codes[w][:, features].bitcast(FP8X4),
-                    lhsT_scale=w_scales[:, scale_columns],
-                    rhs=x_codes[:, nodes].bitcast(FP8X4),
-                    rhs_scale=x_scales[:, nodes],
-                    start=True,
-                    stop=True,
-                )
-                if on_vector:
-                    nc.vector.tensor_copy(window[:, nodes], acc[:, :width])
-                else:
-                    nc.scalar.copy(window[:, nodes], acc[:, :width])
-            return window
+        windows = {
+            (w, block): keep.tile([P, S], F32, name=f"window{w}_{block}") for w in range(3) for block in range(N // P)
+        }
 
-        y = [product(0, 0, plane0, FIRST_PRODUCT_CUTS), product(0, 1, plane3, LATER_PRODUCT_CUTS)]
-        e = [product(1, block, e_windows[block], LATER_PRODUCT_CUTS) for block in range(N // P)]
-        h = [product(2, block, h_windows[block], LATER_PRODUCT_CUTS) for block in range(N // P)]
+        def multiply(w, block, first, width):
+            acc = psum.tile([P, BANK], F32, name="bank", bufs=BANKS)
+            nc.tensor.matmul_mx(
+                out=acc[:, :width],
+                lhsT=w_codes[w][:, block * P : (block + 1) * P].bitcast(FP8X4),
+                lhsT_scale=w_scales[:, w * N + block * P : w * N + (block + 1) * P],
+                rhs=x_codes[:, first : first + width].bitcast(FP8X4),
+                rhs_scale=x_scales[:, first : first + width],
+                start=True,
+                stop=True,
+            )
+            return (acc[:, :width], windows[w, block][:, first : first + width])
 
-        y_at_dst = []
-        for block in range(N // P):
-            gathered = keep.tile([P, U], F32, name=f"y_at_dst{block}")
-            nc.vector.tensor_copy(gathered[:], y[block][:].indirect(dst_tile[:]))
-            y_at_dst.append(gathered)
+        def empty_on_scalar(product):
+            nc.scalar.copy(product[1], product[0])
 
-        gates = keep.tile([P, (N // P) * U], F32, name="gates", tag="codes_then_gates", align_bytes=64)
-        for block in range(N // P):
-            both_ends = keep.tile([P, U], F32, name=f"both_ends{block}")
-            nc.vector.tensor_tensor(both_ends[:], e[block][:].indirect(src_tile[:]), y_at_dst[block][:], ADD)
-            nc.scalar.activation(gates[:, block * U : (block + 1) * U], both_ends[:], TANH)
+        def empty_on_vector(product):
+            nc.vector.tensor_copy(product[1], product[0])
 
-        for block, cuts in enumerate(OUT_CUTS):
-            for first, width in with_starts(cuts):
-                message = keep.tile([P, width], F32, name=f"message{block}_{first}")
-                nc.vector.tensor_tensor(
-                    message[:],
-                    h[block][:].indirect(entries(src_tile, first, width)),
-                    gates[:, block * U + first : block * U + first + width],
-                    MULT,
-                )
-                nc.sync.dma_start(out[block * P : (block + 1) * P, first : first + width], message[:])
+        y_at_dst = [keep.tile([P, U], F32, name=f"y_at_dst{block}") for block in range(N // P)]
+        both_ends = [keep.tile([P, U], F32, name=f"both_ends{block}") for block in range(N // P)]
+        gates = [keep.tile([P, U], F32, name=f"gates{block}") for block in range(N // P)]
+
+        def fetch_y(block, first, width):
+            nc.scalar.activation(
+                y_at_dst[block][:, first : first + width],
+                windows[0, block][:].indirect(entries(dst_tile, first, width)),
+                COPY,
+            )
+
+        def add_e(block, first, width):
+            nc.vector.tensor_tensor(
+                both_ends[block][:, first : first + width],
+                windows[1, block][:].indirect(entries(src_tile, first, width)),
+                y_at_dst[block][:, first : first + width],
+                ADD,
+            )
+
+        def gate(block, first, width):
+            nc.scalar.activation(
+                gates[block][:, first : first + width], both_ends[block][:, first : first + width], TANH
+            )
+
+        def send(block, first, width):
+            message = keep.tile([P, width], F32, name=f"message{block}_{first}")
+            nc.vector.tensor_tensor(
+                message[:],
+                windows[2, block][:].indirect(entries(src_tile, first, width)),
+                gates[block][:, first : first + width],
+                MULT,
+            )
+            nc.sync.dma_start(out[block * P : (block + 1) * P, first : first + width], message[:])
+
+        quarters = with_starts([CUT] * 4)
+        for first, width in quarters:
+            gather_last(first, width)
+        for first, width in ((0, 256), (256, 256), (512, 256), (768, 128), (896, 128)):
+            weave(first, width)
+            quantise(first, width)
+
+        Y, E, H = 0, 1, 2
+        empty_on_scalar(multiply(Y, 0, 0, 256))
+        empty_on_scalar(multiply(Y, 0, 256, 256))
+        empty_on_vector(multiply(Y, 0, 512, 256))
+        empty_on_vector(multiply(Y, 0, 768, 128))
+        empty_on_vector(multiply(Y, 0, 896, 128))
+        empty_on_vector(multiply(E, 0, 0, BANK))
+        empty_on_vector(multiply(E, 0, BANK, BANK))
+        later = {
+            (w, block, first): multiply(w, block, first, BANK)
+            for w, block in ((H, 0), (Y, 1), (E, 1), (H, 1))
+            for first in (0, BANK)
+        }
+
+        for first, width in quarters:
+            fetch_y(0, first, width)
+            add_e(0, first, width)
+        empty_on_scalar(later[H, 0, 0])
+        empty_on_vector(later[H, 0, BANK])
+        gate(0, 0, BANK)
+        empty_on_scalar(later[Y, 1, 0])
+        empty_on_scalar(later[Y, 1, BANK])
+        gate(0, BANK, BANK)
+        send(0, 0, BANK)
+        send(0, BANK, BANK)
+        fetch_y(1, 0, 256)
+        empty_on_scalar(later[E, 1, 0])
+        empty_on_vector(later[E, 1, BANK])
+        add_e(1, 0, 256)
+        fetch_y(1, 256, 256)
+        add_e(1, 256, 256)
+        empty_on_scalar(later[H, 1, 0])
+        empty_on_scalar(later[H, 1, BANK])
+        gate(1, 0, 256)
+        fetch_y(1, 512, 256)
+        send(1, 0, 256)
+        add_e(1, 512, 256)
+        gate(1, 256, 256)
+        fetch_y(1, 768, 256)
+        send(1, 256, 256)
+        add_e(1, 768, 256)
+        gate(1, 512, 256)
+        gate(1, 768, 256)
+        send(1, 512, 256)
+        send(1, 768, 128)
+        send(1, 896, 128)

@@ -166,25 +166,31 @@ def tile_picked_edgeatt_tanh_e_kernel(
             nc.sync.dma_start(out[block * P : (block + 1) * P, first : first + width], message[:])
 
         quarters = with_starts([CUT] * 4)
-        for first, width in quarters:
+        for first, width in quarters[:3]:
             gather_last(first, width)
+        apart_last = keep.tile([P, CUT], BF16, name="apart_last")
+        nc.scalar.activation(apart_last[:], planes[3][:].indirect(entries(offs_tile, S - CUT, CUT)), COPY)
+        nc.vector.tensor_copy(halves[:, 1, S - CUT :, 1], apart_last[:])
         for first, width in ((0, 256), (256, 256), (512, 256), (768, 128), (896, 128)):
             weave(first, width)
             quantise(first, width)
 
         Y, E, H = 0, 1, 2
         empty_on_scalar(multiply(Y, 0, 0, 256))
+        y1_first = multiply(Y, 1, 0, 256)
         empty_on_scalar(multiply(Y, 0, 256, 256))
-        empty_on_vector(multiply(Y, 0, 512, 256))
+        empty_on_scalar(multiply(Y, 0, 512, 256))
+        empty_on_scalar(y1_first)
         empty_on_vector(multiply(Y, 0, 768, 128))
         empty_on_vector(multiply(Y, 0, 896, 128))
         empty_on_vector(multiply(E, 0, 0, BANK))
         empty_on_vector(multiply(E, 0, BANK, BANK))
-        later = {
-            (w, block, first): multiply(w, block, first, BANK)
-            for w, block in ((H, 0), (Y, 1), (E, 1), (H, 1))
-            for first in (0, BANK)
-        }
+        later = {(H, 0, first): multiply(H, 0, first, BANK) for first in (0, BANK)}
+        later[Y, 1, 0] = multiply(Y, 1, 256, 256)
+        later[Y, 1, BANK] = multiply(Y, 1, BANK, BANK)
+        for w in (E, H):
+            for first in (0, BANK):
+                later[w, 1, first] = multiply(w, 1, first, BANK)
 
         for first, width in quarters:
             fetch_y(0, first, width)

@@ -59,22 +59,34 @@ def tile_picked_edgeatt_tanh_e_kernel(
         for j in (0, 1, 3):
             nc.sync.dma_start(planes[j][:], x_planes[:, j, :])
 
-        def load_weight(w, words, scales):
-            codes = keep.tile([P, N], U32, name=f"w_codes{w}", align_bytes=64)
-            nc.sync.dma_start(codes[:].bitcast(I32), words[0].rearrange("p n t -> p (n t)").bitcast(I32))
+        def load_codes(name, words, first, width):
+            codes = keep.tile([P, width], U32, name=name, tag=name, align_bytes=64)
+            nc.sync.dma_start(
+                codes[:].bitcast(I32), words[0].rearrange("p n t -> p (n t)").bitcast(I32)[:, first : first + width]
+            )
+            return codes
+
+        def load_scales(w, scales):
             for q in range(P // QUADRANT):
                 nc.sync.dma_start(
                     w_scales[QUADRANT * q : QUADRANT * q + SCALE_ROWS, w * N : (w + 1) * N].bitcast(I32),
                     scales[0, SCALE_ROWS * q : SCALE_ROWS * (q + 1), :].bitcast(I32),
                 )
-            return codes
 
-        w1_codes = load_weight(0, w1_words, w1_scales)
-        w2_codes = load_weight(1, w2_words, w2_scales)
+        w1_codes = load_codes("w1_codes", w1_words, 0, N)
+        load_scales(0, w1_scales)
+        w2_codes = load_codes("w2_codes", w2_words, 0, N)
+        load_scales(1, w2_scales)
         nc.sync.dma_start(dst_tile[:], dst)
-        w3_codes = load_weight(2, w3_words, w3_scales)
         nc.sync.dma_start(src_tile[:], src)
-        w_codes = (w1_codes, w2_codes, w3_codes)
+        w3_codes0 = load_codes("w3_codes0", w3_words, 0, P)
+        load_scales(2, w3_scales)
+        w3_codes1 = load_codes("w3_codes1", w3_words, P, P)
+        w_codes = (
+            (w1_codes[:, :P], w1_codes[:, P:]),
+            (w2_codes[:, :P], w2_codes[:, P:]),
+            (w3_codes0[:], w3_codes1[:]),
+        )
 
         woven = keep.tile([P, S * PLANES], BF16, name="woven", align_bytes=64)
         picked = keep.tile([P, 2 * S], U32, name="picked")
@@ -116,7 +128,7 @@ def tile_picked_edgeatt_tanh_e_kernel(
             acc = psum.tile([P, BANK], F32, name="bank", bufs=BANKS)
             nc.tensor.matmul_mx(
                 out=acc[:, :width],
-                lhsT=w_codes[w][:, block * P : (block + 1) * P].bitcast(FP8X4),
+                lhsT=w_codes[w][block].bitcast(FP8X4),
                 lhsT_scale=w_scales[:, w * N + block * P : w * N + (block + 1) * P],
                 rhs=x_codes[:, first : first + width].bitcast(FP8X4),
                 rhs_scale=x_scales[:, first : first + width],
@@ -133,7 +145,7 @@ def tile_picked_edgeatt_tanh_e_kernel(
 
         y_at_dst = [keep.tile([P, U], F32, name=f"y_at_dst{block}") for block in range(N // P)]
         both_ends = [keep.tile([P, U], F32, name=f"both_ends{block}") for block in range(N // P)]
-        gates = [keep.tile([P, U], F32, name=f"gates{block}") for block in range(N // P)]
+        gates = []
 
         def fetch_y(block, first, width):
             nc.scalar.activation(
@@ -192,6 +204,8 @@ def tile_picked_edgeatt_tanh_e_kernel(
             for first in (0, BANK):
                 later[w, 1, first] = multiply(w, 1, first, BANK)
 
+        gates.append(keep.tile([P, U], F32, name="gates0", tag="w3_codes0", align_bytes=64))
+        gates.append(keep.tile([P, U], F32, name="gates1"))
         for first, width in quarters:
             fetch_y(0, first, width)
             add_e(0, first, width)

@@ -227,14 +227,18 @@ def tile_picked_edgeatt_tanh_e_kernel(
         empty_on_scalar(later[H, 1, BANK])
         gate(1, 0, 256)
         fetch_y(1, 512, 256)
+        fetch_y(1, 768, 256)
         send(1, 0, 256)
         add_e(1, 512, 256)
-        gate(1, 256, 256)
-        fetch_y(1, 768, 256)
-        send(1, 256, 256)
         add_e(1, 768, 256)
+        gate(1, 256, 256)
+        send(1, 256, 256)
+        h_at_src = keep.tile([P, 256], F32, name="h_at_src")
+        nc.scalar.activation(h_at_src[:], windows[H, 1][:].indirect(entries(src_tile, 512, 256)), COPY)
         gate(1, 512, 256)
         gate(1, 768, 256)
-        send(1, 512, 256)
+        plain = keep.tile([P, 256], F32, name="plain")
+        nc.vector.tensor_tensor(plain[:], h_at_src[:], gates[1][:, 512:768], MULT)
+        nc.sync.dma_start(out[P:, 512:768], plain[:])
         send(1, 768, 128)
         send(1, 896, 128)

@@ -206,9 +206,11 @@ def tile_picked_edgeatt_tanh_e_kernel(
 
         gates.append(keep.tile([P, U], F32, name="gates0", tag="w3_codes0", align_bytes=64))
         gates.append(keep.tile([P, U], F32, name="gates1"))
-        for first, width in quarters:
+        nc.vector.tensor_copy(y_at_dst[0][:, 896:], windows[Y, 0][:].indirect(entries(dst_tile, 896, 128)))
+        for first, width in with_starts([256, 256, 384]):
             fetch_y(0, first, width)
-            add_e(0, first, width)
+        for first in (0, BANK):
+            add_e(0, first, BANK)
         empty_on_scalar(later[H, 0, 0])
         empty_on_vector(later[H, 0, BANK])
         gate(0, 0, BANK)

@@ -213,25 +213,24 @@ def tile_picked_edgeatt_tanh_e_kernel(
             add_e(0, first, BANK)
         empty_on_scalar(later[H, 0, 0])
         empty_on_vector(later[H, 0, BANK])
-        gate(0, 0, BANK)
         empty_on_scalar(later[Y, 1, 0])
+        gate(0, 0, BANK)
         empty_on_scalar(later[Y, 1, BANK])
         gate(0, BANK, BANK)
         send(0, 0, BANK)
         send(0, BANK, BANK)
-        fetch_y(1, 0, 256)
+        fetch_y(1, 0, BANK)
         empty_on_scalar(later[E, 1, 0])
         empty_on_vector(later[E, 1, BANK])
         add_e(1, 0, 256)
-        fetch_y(1, 256, 256)
         add_e(1, 256, 256)
         empty_on_scalar(later[H, 1, 0])
         empty_on_scalar(later[H, 1, BANK])
-        gate(1, 0, 256)
         fetch_y(1, 512, 256)
+        add_e(1, 512, 256)
+        gate(1, 0, 256)
         fetch_y(1, 768, 256)
         send(1, 0, 256)
-        add_e(1, 512, 256)
         add_e(1, 768, 256)
         gate(1, 256, 256)
         send(1, 256, 256)
@@ -243,4 +242,8 @@ def tile_picked_edgeatt_tanh_e_kernel(
         nc.vector.tensor_tensor(plain[:], h_at_src[:], gates[1][:, 512:768], MULT)
         nc.sync.dma_start(out[P:, 512:768], plain[:])
         send(1, 768, 128)
-        send(1, 896, 128)
+        h_last = keep.tile([P, 128], F32, name="h_last")
+        nc.scalar.activation(h_last[:], windows[H, 1][:].indirect(entries(src_tile, 896, 128)), COPY)
+        plain_last = keep.tile([P, 128], F32, name="plain_last")
+        nc.vector.tensor_tensor(plain_last[:], h_last[:], gates[1][:, 896:], MULT)
+        nc.sync.dma_start(out[P:, 896:], plain_last[:])

@@ -195,8 +195,8 @@ def tile_picked_edgeatt_tanh_e_kernel(
         empty_on_scalar(y1_first)
         empty_on_vector(multiply(Y, 0, 768, 128))
         empty_on_vector(multiply(Y, 0, 896, 128))
-        empty_on_vector(multiply(E, 0, 0, BANK))
-        empty_on_vector(multiply(E, 0, BANK, BANK))
+        for first, width in quarters:
+            empty_on_vector(multiply(E, 0, first, width))
         later = {(H, 0, first): multiply(H, 0, first, BANK) for first in (0, BANK)}
         later[Y, 1, 0] = multiply(Y, 1, 256, 256)
         later[Y, 1, BANK] = multiply(Y, 1, BANK, BANK)
@@ -206,19 +206,19 @@ def tile_picked_edgeatt_tanh_e_kernel(
 
         gates.append(keep.tile([P, U], F32, name="gates0", tag="w3_codes0", align_bytes=64))
         gates.append(keep.tile([P, U], F32, name="gates1"))
-        nc.vector.tensor_copy(y_at_dst[0][:, 896:], windows[Y, 0][:].indirect(entries(dst_tile, 896, 128)))
-        for first, width in with_starts([256, 256, 384]):
+        nc.vector.tensor_copy(y_at_dst[0][:, 832:], windows[Y, 0][:].indirect(entries(dst_tile, 832, 192)))
+        for first, width in with_starts([448, 384]):
             fetch_y(0, first, width)
-        for first in (0, BANK):
-            add_e(0, first, BANK)
+        for first, width in with_starts([448, 576]):
+            add_e(0, first, width)
         empty_on_scalar(later[H, 0, 0])
         empty_on_vector(later[H, 0, BANK])
         empty_on_scalar(later[Y, 1, 0])
-        gate(0, 0, BANK)
+        gate(0, 0, 448)
         empty_on_scalar(later[Y, 1, BANK])
-        gate(0, BANK, BANK)
-        send(0, 0, BANK)
-        send(0, BANK, BANK)
+        gate(0, 448, 576)
+        send(0, 0, 448)
+        send(0, 448, 576)
         fetch_y(1, 0, BANK)
         empty_on_scalar(later[E, 1, 0])
         empty_on_vector(later[E, 1, BANK])

@@ -219,15 +219,14 @@ def tile_picked_edgeatt_tanh_e_kernel(
         gate(0, 448, 576)
         send(0, 0, 448)
         send(0, 448, 576)
-        fetch_y(1, 0, BANK)
+        fetch_y(1, 0, 384)
         empty_on_scalar(later[E, 1, 0])
         empty_on_vector(later[E, 1, BANK])
-        add_e(1, 0, 256)
-        add_e(1, 256, 256)
+        add_e(1, 0, 384)
+        fetch_y(1, 384, 384)
+        add_e(1, 384, 384)
         empty_on_scalar(later[H, 1, 0])
         empty_on_scalar(later[H, 1, BANK])
-        fetch_y(1, 512, 256)
-        add_e(1, 512, 256)
         gate(1, 0, 256)
         fetch_y(1, 768, 256)
         send(1, 0, 256)

from contextlib import ExitStack

import concourse.mybir as mybir

K, T, S, N, U = 512, 2048, 1024, 256, 1024
FLOPS = 3 * 2 * K * N * S

F32 = mybir.dt.float32
BF16 = mybir.dt.bfloat16
I32 = mybir.dt.int32
U32 = mybir.dt.uint32
U16 = mybir.dt.uint16
U8 = mybir.dt.uint8
FP8X4 = mybir.dt.float8_e4m3fn_x4
ADD = mybir.AluOpType.add
MULT = mybir.AluOpType.mult
TANH = mybir.ActivationFunctionType.Tanh
COPY = mybir.ActivationFunctionType.Copy

P = 128
PLANES = 4
ENTRIES_PER_COLUMN = 16
QUADRANT = 32
SCALE_ROWS = 4
BANK = 512
BANKS = 8

SCALAR_SHARE = 256
CUT = 256


def entries(list_tile, first, count):
    return list_tile[:, first // ENTRIES_PER_COLUMN : (first + count) // ENTRIES_PER_COLUMN]


def with_starts(widths):
    return [(sum(widths[:i]), width) for i, width in enumerate(widths)]


def tile_picked_edgeatt_tanh_e_kernel(
    tc, xT, w1_words, w1_scales, w2_words, w2_scales, w3_words, w3_scales, offs, src, dst, out
):
    nc = tc.nc
    with ExitStack() as ctx:
        keep = ctx.enter_context(tc.tile_pool(name="keep", bufs=1))
        psum = ctx.enter_context(tc.psum_pool(name="psum", bufs=1))

        offs_tile = keep.tile([P, S // ENTRIES_PER_COLUMN], U16, name="offs_tile")
        src_tile = keep.tile([P, U // ENTRIES_PER_COLUMN], U16, name="src_tile")
        dst_tile = keep.tile([P, U // ENTRIES_PER_COLUMN], U16, name="dst_tile")

        w_scales = keep.tile([P, 3 * N], U8, name="w_scales", align_bytes=64)
        nc.vector.memset(w_scales[:].bitcast(I32), 0)

        x_planes = xT.rearrange("(p j) t -> p j t", j=PLANES)
        planes = [keep.tile([P, T], F32, name=f"plane{j}") for j in range(PLANES)]
        nc.sync.dma_start(planes[2][:], x_planes[:, 2, :])
        nc.sync.dma_start(offs_tile[:], offs)
        for j in (0, 1, 3):
            nc.sync.dma_start(planes[j][:], x_planes[:, j, :])

        def load_codes(name, words, first, width):
            codes = keep.tile([P, width], U32, name=name, tag=name, align_bytes=64)
            nc.sync.dma_start(
                codes[:].bitcast(I32), words[0].rearrange("p n t -> p (n t)").bitcast(I32)[:, first : first + width]
            )
            return codes

        def load_scales(w, scales):
            for q in range(P // QUADRANT):
                nc.sync.dma_start(
                    w_scales[QUADRANT * q : QUADRANT * q + SCALE_ROWS, w * N : (w + 1) * N].bitcast(I32),
                    scales[0, SCALE_ROWS * q : SCALE_ROWS * (q + 1), :].bitcast(I32),
                )

        w1_codes = load_codes("w1_codes", w1_words, 0, N)
        load_scales(0, w1_scales)
        w2_codes = load_codes("w2_codes", w2_words, 0, N)
        load_scales(1, w2_scales)
        nc.sync.dma_start(dst_tile[:], dst)
        nc.sync.dma_start(src_tile[:], src)
        w3_codes0 = load_codes("w3_codes0", w3_words, 0, P)
        load_scales(2, w3_scales)
        w3_codes1 = load_codes("w3_codes1", w3_words, P, P)
        w_codes = (
            (w1_codes[:, :P], w1_codes[:, P:]),
            (w2_codes[:, :P], w2_codes[:, P:]),
            (w3_codes0[:], w3_codes1[:]),
        )

        woven = keep.tile([P, S * PLANES], BF16, name="woven", align_bytes=64)
        picked = keep.tile([P, 2 * S], U32, name="picked")
        halves = picked[:].bitcast(BF16).rearrange("p (u n e) -> p u n e", u=2, e=2)
        own = S - SCALAR_SHARE
        apart = keep.tile([P, 2, SCALAR_SHARE], BF16, name="apart")

        nc.vector.tensor_copy(halves[:, 1, :, 0], planes[2][:].indirect(offs_tile[:]))
        for j in (0, 1):
            nc.vector.tensor_copy(halves[:, 0, :own, j], planes[j][:].indirect(entries(offs_tile, 0, own)))
            nc.scalar.activation(apart[:, j, :], planes[j][:].indirect(entries(offs_tile, own, SCALAR_SHARE)), COPY)
        nc.scalar.copy(halves[:, 0, own:, :], apart[:].rearrange("p e n -> p n e"))

        by_pair = picked[:].rearrange("p (u n) -> p n u", u=2)
        woven_words = woven[:].bitcast(U32).rearrange("p (n u) -> p n u", u=2)
        x_codes = keep.tile([P, S], U32, name="x_codes", align_bytes=64)
        x_scales = keep.tile([P, S], U8, name="x_scales", align_bytes=64)

        def gather_last(first, width):
            nc.vector.tensor_copy(
                halves[:, 1, first : first + width, 1], planes[3][:].indirect(entries(offs_tile, first, width))
            )

        def weave(first, width):
            nc.scalar.copy(woven_words[:, first : first + width, :], by_pair[:, first : first + width, :])

        def quantise(first, width):
            nc.vector.quantize_mx(
                out=x_codes[:, first : first + width].bitcast(FP8X4),
                scales=x_scales[:, first : first + width],
                in_=woven[:, first * PLANES : (first + width) * PLANES],
            )

        windows = {
            (w, block): keep.tile([P, S], F32, name=f"window{w}_{block}") for w in range(3) for block in range(N // P)
        }

        def multiply(w, block, first, width):
            acc = psum.tile([P, BANK], F32, name="bank", bufs=BANKS)
            nc.tensor.matmul_mx(
                out=acc[:, :width],
                lhsT=w_codes[w][block].bitcast(FP8X4),
                lhsT_scale=w_scales[:, w * N + block * P : w * N + (block + 1) * P],
                rhs=x_codes[:, first : first + width].bitcast(FP8X4),
                rhs_scale=x_scales[:, first : first + width],
                start=True,
                stop=True,
            )
            return (acc[:, :width], windows[w, block][:, first : first + width])

        def empty_on_scalar(product):
            nc.scalar.copy(product[1], product[0])

        def empty_on_vector(product):
            nc.vector.tensor_copy(product[1], product[0])

        y_at_dst = [keep.tile([P, U], F32, name=f"y_at_dst{block}") for block in range(N // P)]
        both_ends = [keep.tile([P, U], F32, name=f"both_ends{block}") for block in range(N // P)]
        gates = []

        def fetch_y(block, first, width):
            nc.scalar.activation(
                y_at_dst[block][:, first : first + width],
                windows[0, block][:].indirect(entries(dst_tile, first, width)),
                COPY,
            )

        def add_e(block, first, width):
            nc.vector.tensor_tensor(
                both_ends[block][:, first : first + width],
                windows[1, block][:].indirect(entries(src_tile, first, width)),
                y_at_dst[block][:, first : first + width],
                ADD,
            )

        def gate(block, first, width):
            nc.scalar.activation(
                gates[block][:, first : first + width], both_ends[block][:, first : first + width], TANH
            )

        def send(block, first, width):
            message = keep.tile([P, width], F32, name=f"message{block}_{first}")
            nc.vector.tensor_tensor(
                message[:],
                windows[2, block][:].indirect(entries(src_tile, first, width)),
                gates[block][:, first : first + width],
                MULT,
            )
            nc.sync.dma_start(out[block * P : (block + 1) * P, first : first + width], message[:])

        quarters = with_starts([CUT] * 4)
        for first, width in quarters[:3]:
            gather_last(first, width)
        apart_last = keep.tile([P, CUT], BF16, name="apart_last")
        nc.scalar.activation(apart_last[:], planes[3][:].indirect(entries(offs_tile, S - CUT, CUT)), COPY)
        nc.vector.tensor_copy(halves[:, 1, S - CUT :, 1], apart_last[:])
        for first, width in ((0, 256), (256, 256), (512, 256), (768, 128), (896, 128)):
            weave(first, width)
            quantise(first, width)

        Y, E, H = 0, 1, 2
        empty_on_scalar(multiply(Y, 0, 0, 256))
        y1_first = multiply(Y, 1, 0, 256)
        empty_on_scalar(multiply(Y, 0, 256, 256))
        empty_on_scalar(multiply(Y, 0, 512, 256))
        empty_on_scalar(y1_first)
        empty_on_vector(multiply(Y, 0, 768, 128))
        empty_on_vector(multiply(Y, 0, 896, 128))
        for first, width in quarters:
            empty_on_vector(multiply(E, 0, first, width))
        later = {(H, 0, first): multiply(H, 0, first, BANK) for first in (0, BANK)}
        later[Y, 1, 0] = multiply(Y, 1, 256, 256)
        later[Y, 1, BANK] = multiply(Y, 1, BANK, BANK)
        for w in (E, H):
            for first in (0, BANK):
                later[w, 1, first] = multiply(w, 1, first, BANK)

        gates.append(keep.tile([P, U], F32, name="gates0", tag="w3_codes0", align_bytes=64))
        gates.append(keep.tile([P, U], F32, name="gates1"))
        nc.vector.tensor_copy(y_at_dst[0][:, 832:], windows[Y, 0][:].indirect(entries(dst_tile, 832, 192)))
        for first, width in with_starts([448, 384]):
            fetch_y(0, first, width)
        for first, width in with_starts([448, 576]):
            add_e(0, first, width)
        empty_on_scalar(later[H, 0, 0])
        empty_on_vector(later[H, 0, BANK])
        empty_on_scalar(later[Y, 1, 0])
        gate(0, 0, 448)
        empty_on_scalar(later[Y, 1, BANK])
        gate(0, 448, 576)
        send(0, 0, 448)
        send(0, 448, 576)
        fetch_y(1, 0, 384)
        empty_on_scalar(later[E, 1, 0])
        empty_on_vector(later[E, 1, BANK])
        add_e(1, 0, 384)
        fetch_y(1, 384, 384)
        add_e(1, 384, 384)
        empty_on_scalar(later[H, 1, 0])
        empty_on_scalar(later[H, 1, BANK])
        gate(1, 0, 256)
        fetch_y(1, 768, 256)
        send(1, 0, 256)
        add_e(1, 768, 256)
        gate(1, 256, 256)
        send(1, 256, 256)
        h_at_src = keep.tile([P, 256], F32, name="h_at_src")
        nc.scalar.activation(h_at_src[:], windows[H, 1][:].indirect(entries(src_tile, 512, 256)), COPY)
        gate(1, 512, 256)
        gate(1, 768, 256)
        plain = keep.tile([P, 256], F32, name="plain")
        nc.vector.tensor_tensor(plain[:], h_at_src[:], gates[1][:, 512:768], MULT)
        nc.sync.dma_start(out[P:, 512:768], plain[:])
        send(1, 768, 128)
        h_last = keep.tile([P, 128], F32, name="h_last")
        nc.scalar.activation(h_last[:], windows[H, 1][:].indirect(entries(src_tile, 896, 128)), COPY)
        plain_last = keep.tile([P, 128], F32, name="plain_last")
        nc.vector.tensor_tensor(plain_last[:], h_last[:], gates[1][:, 896:], MULT)
        nc.sync.dma_start(out[P:, 896:], plain_last[:])
